import numpy as np, ml_dtypes
CORES = [48,51,52,55]
N = 4
import mx_ref
BF = ml_dtypes.bfloat16
def gentries(a):
    return np.ascontiguousarray(a.reshape(8, 16, -1).transpose(0, 2, 1)).reshape(8, -1)
def gtable(e):
    e = np.asarray(e); return np.ascontiguousarray(e.reshape(8, -1, 16).transpose(0, 2, 1)).reshape(128, -1).astype(np.int32)
def gcols(t, e):
    v = np.concatenate([t.reshape(8, 16, -1, 4), np.zeros((8, 16, 1, 4), BF)], axis=2)
    return np.ascontiguousarray(np.stack([v[g][:, e[g]] for g in range(8)])).reshape(128, -1)
def tile(rs):
    return np.stack(rs, axis=2).reshape(128, -1).astype(BF)
def pick(q, e):
    c = np.concatenate([q[0].reshape(128, -1, 4), np.zeros((128, 1, 4), np.uint8)], axis=1); s = np.concatenate([q[1], np.ones((16, 1), np.uint8)], axis=1)
    return (np.ascontiguousarray(c[:, e].reshape(128, -1)), np.ascontiguousarray(s[:, e]))
def join(*qs):
    return (np.concatenate([q[0] for q in qs], axis=1), np.concatenate([q[1] for q in qs], axis=1))
def put(q, e, v):
    c, s = q[0].reshape(128, -1, 4).copy(), q[1].copy(); c[:, e] = v[0].reshape(128, -1, 4); s[:, e] = v[1]
    return (c.reshape(128, -1), s)
def pk(c, s):
    return (np.ascontiguousarray(c), mx_ref.live(s))
def emit(q):
    return q[0], q[1]
def packed(v, rng):
    q = [mx_ref.quantize(np.ascontiguousarray(v[r])) for r in range(N)]
    return np.stack([a for a, b in q]), np.stack([mx_ref.plane(b, rng) for a, b in q])
def values_of_codes():
    e, c = np.zeros((128, 128, 4), np.float32), np.zeros((128, 2, 4), np.uint8)
    e[np.arange(128), np.arange(128), 0] = 1
    c[:127, :, 0] = np.arange(256).reshape(2, 128).T[:127]
    return mx_ref.matmul(mx_ref.quantize(e.reshape(128, 512).astype(BF)), (c.reshape(128, 8), np.full((16, 2), 127, np.uint8))).T.reshape(-1).astype(np.float64)
CODE_VALUE, SCALE_VALUE = values_of_codes(), 2.0 ** (np.arange(256) - 127.0)
def decode(q):
    return (CODE_VALUE[q[0]].reshape(16, 8, -1, 4) * SCALE_VALUE[q[1]][:, None, :, None] + 0.0).reshape(128, -1).astype(np.float32)
def f(rng, *shape):
    return mx_ref.flush((rng.standard_normal(shape, dtype=np.float32) * np.exp2(rng.integers(-2, 3, shape[:-1] + (1,)))).astype(BF))
def wide(rng, *shape, cols=0):
    v = rng.standard_normal(shape, dtype=np.float32) * np.exp2(rng.integers(-12, 13, shape)).astype(np.float32)
    if cols: v *= np.repeat(np.exp2(rng.integers(-cols, cols + 1, shape[:-2] + (1, shape[-1] // 4))) * (rng.random(shape[:-2] + (1, shape[-1] // 4)) > 0.0625), 4, axis=-1).astype(np.float32)
    return mx_ref.flush(v.astype(BF))
C, H = 448, 224
STEP = [1, 2, 3]
PLACES = np.arange(C)
def numbers_of(rng):
    return {"x": np.array(f(rng, N, 128, 4 * C)), "u": np.array(f(rng, N, 128, 512)), "v": np.array(f(rng, N, 128, 512))}
def drawn(rng):
    o = rng.permuted(np.tile(PLACES, (N, 8, 3, 1)), axis=3)
    k = np.zeros_like(o)
    np.put_along_axis(k, o, o.reshape(N, 8, 3, H, 2)[..., ::-1].reshape(N, 8, 3, C), axis=3)
    e = np.tile(PLACES, (N, 8, 1))
    return rng.permuted(e, axis=2), rng.permuted(e, axis=2), k
def stored(p, e, k):
    return {"pp": np.stack([gtable(p[r]) for r in range(N)]), "rf": np.stack([gtable(e[r]) for r in range(N)]), "pr": np.stack([gtable(k[r].reshape(8, 3 * C)) for r in range(N)])}
def layers(rng, still=[]):
    w = np.array(f(rng, N, 128, 2048)).reshape(N, 8, 16, 4, 8, 16, 4)
    for i in still:
        w[:, :, i] = 0
        w[:, :, :, :, :, i] = 0
    return w
def weights(rng, w):
    c, s = packed(np.ascontiguousarray(w).reshape(N, 128, 2048), rng)
    return {"wc": c, "ws": s}
def scoring(d):
    u = d["u"].reshape(N, 128, 128, 4)
    u[:, :, ::16] = 0
    u[:, :, 1::16] = 0
    return u
def setup_inputs(rng):
    return {**numbers_of(rng), **stored(*drawn(rng)), **weights(rng, layers(rng))}
def setup_inputs_ties(rng):
    d = numbers_of(rng)
    p, e, k = drawn(rng)
    o = rng.permutation(N)
    k[o[3], :4] = k[o[3], :4, :1]
    a, b = rng.integers(-1, 2, (2, N, 8, C))
    a[o[0]] = 0
    a[o[1]] = 1
    b[o[1], :4] = 1
    b[o[1], 4:] = 0
    for g in range(4): a[o[3], g, p[o[3], g]] = np.where(PLACES < k[o[3], g, 0], 1, -rng.integers(0, 2, C))
    x = d["x"].reshape(N, 8, 16, C, 4)
    x[:, :, 0] = 0
    x[:, :, 0, :, 0] = a.astype(np.float32).astype(BF)
    x[:, :, 0, :, 1] = b.astype(np.float32).astype(BF)
    u = scoring(d)
    for h in range(0, 128, 16):
        u[:, h, h, 0] = 1
        u[:, h, h + 1, 1] = 1
    return {"x": x.reshape(N, 128, 4 * C), "u": u.reshape(N, 128, 512), "v": d["v"], **stored(p, rng.integers(0, C, (N, 8, C)), k), **weights(rng, layers(rng, [0]))}
def setup_inputs_near(rng):
    d = numbers_of(rng)
    o = rng.permutation(N)
    z = int(np.argmax(o))
    k = np.where(o % 2 == 0, 2.0 ** -30, 1.0)
    x = np.zeros((N, 8, 16, C, 4))
    for i in (0, 2):
        s = rng.integers(-1, 2, (N, 8, C)) * k[:, None, None]
        x[:, :, i, :, 0] = 1.125 * s
        x[:, :, i + 1, :, 0] = -1.25 * s
    for r in range(N):
        at_ = [0, C - 1, int(rng.integers(C)), int(rng.integers(C))]
        for g, j in zip(rng.permutation(8)[:4], at_): x[r, g, 0, j, 0] = 2.0 ** 30 * rng.choice([-1.0, 1.0])
    x[:, :, 8:] = rng.choice([-1.0, 1.0], (N, 8, 8, C, 4)) * (1 + 0.125 * rng.integers(0, 8, (N, 8, 8, C, 4))) * 2.0 ** -30
    x[z, :, :8] = 0
    x[:, :, 7, :, 0] = 2.0 ** -30
    x[:, :, 8, :, 3] = 2.0 ** -30
    u = scoring(d)
    w = layers(rng)
    w[:, :, :8] = 0
    w[:, :, :, :, :, :9] = 0
    for h in range(0, 128, 16):
        for i in (0, 1):
            u[:, h + 2 * i, h + i, 0] = (1.125 * k).astype(np.float32).astype(BF)
            u[:, h + 2 * i + 1, h + i, 0] = k.astype(np.float32).astype(BF)
            u[z, :, h + i] = 0
            u[z, h + 5 + i, h + i, 0] = 2.0 ** -30
            w[z, h // 16, 8, 0, h // 16, 5 + i, i] = 2.0 ** -8
    return {"x": x.astype(np.float32).reshape(N, 128, 4 * C).astype(BF), "u": u.reshape(N, 128, 512), "v": d["v"], **stored(*drawn(rng)), **weights(rng, w)}
def setup_inputs_odd(rng):
    d = numbers_of(rng)
    x = (2 * rng.integers(0, 8, (N, 16, 8, C, 4)) + 1) * 2.0 ** -8 * rng.choice([-1.0, 1.0], (N, 16, 8, C, 4))
    x[:, :, 0, :, 0] = 2.0 ** 8 * np.where(rng.random((N, 16, C)) < 0.5, 1.96875, 1.875)
    u = scoring(d)
    for i in (0, 1):
        x[:, ::2, 1 + 2 * i, :, 0] = (8 + rng.integers(0, 2, (N, 8, C))) * 2.0 ** -8
        x[:, ::2, 2 + 2 * i, :, 0] = 8 * 2.0 ** -8
        for h in range(0, 128, 16):
            u[:, h + 1 + 2 * i, h + i, 0] = 1
            u[:, h + 2 + 2 * i, h + i, 0] = -1
    return {"x": x.astype(np.float32).reshape(N, 128, 4 * C).astype(BF), "u": u.reshape(N, 128, 512), "v": d["v"], **stored(*drawn(rng)), **weights(rng, layers(rng, [0, 1, 2, 3, 4, 8]))}
def setup_inputs_ends(rng):
    d = numbers_of(rng)
    p, q, k = drawn(rng)
    o, e = rng.permutation(N) % 4, rng.permutation(N) % 4
    s = rng.choice([-1.0, 1.0], (N, 128, C, 4))
    s[o == 0] = -1
    s[o == 1] = rng.choice([-1.0, 1.0], (N, 1, C, 1))[o == 1]
    x = s * (0.87 + 0.07 * rng.random((N, 128, C, 4))) * 2.0 ** 30
    x[:, 15::16] = 0
    x[o == 3] = 2.0 ** -30
    size = np.where(o == 3, 2.0 ** -30, 2.0 ** 30)
    u = scoring(d)
    for i in (0, 1):
        a = np.stack([rng.permutation(8) % 2 * 2.0 - 1.0 for r in range(N)]) * size[:, None]
        u[:, :, i::16] = a.astype(np.float32).astype(BF)[:, None, :, None]
    v = rng.choice([-1.0, 1.0], (N, 128, 512)) * np.where(o % 2 == 1, 2.0 ** -30, 2.0 ** 30)[:, None, None]
    p[e == 0] = PLACES
    p[e == 1] = PLACES[::-1]
    q[e == 0] = np.where(np.arange(8) % 2 == 0, C - 1, 0)[:, None]
    q[e == 1] = (rng.integers(0, 2, (N, 8, C)) * (C - 1))[e == 1]
    q[e == 2] = PLACES
    q[e == 3] = rng.integers(0, C, (N, 8, C))[e == 3]
    k[e == 0] = PLACES
    k[e == 1] = PLACES[::-1]
    k[e == 2] = PLACES ^ 1
    w = np.zeros((N, 128, 4, 128, 4), np.float32)
    i = np.arange(128)
    for b in range(4): w[:, i, b, i, b] = np.where(o[:, None] == 3, np.where(i % 16 == 15, 2.0 ** 8, 2.0 ** -8), -0.25)
    return {"x": x.astype(np.float32).reshape(N, 128, 4 * C).astype(BF), "u": u.reshape(N, 128, 512), "v": v.astype(np.float32).astype(BF), **stored(p, q, k), **weights(rng, w.astype(BF))}
def setup_inputs_spread(rng):
    d = setup_inputs(rng)
    d["x"] = wide(rng, N, 128, 4 * C, cols=6)
    return d
def check_inputs(d):
    b = []
    for k in ("x", "u", "v"):
        a = np.abs(d[k].astype(np.float32))
        if not (np.isfinite(a).all() and ((a == 0) | (a >= 2.0 ** -30) & (a <= 2.0 ** 30)).all()): b.append("a value of " + k)
    for k in ("pp", "rf", "pr"):
        if not ((d[k] >= 0) & (d[k] < C)).all(): b.append("an entry of " + k)
    none, least, most = [emit(mx_ref.quantize(np.full((128, 16), k, np.float32).astype(BF)))[1][0, 0] for k in (0.0, 2.0 ** -8, 2.0 ** 8)]
    for r in range(N):
        if not (np.sort(gentries(d["pp"][r]), axis=1) == PLACES).all(): b.append("pp: a column not once in a group")
        k = gentries(d["pr"][r]).reshape(8, 3, C)
        if ((k >= 0) & (k < C)).all() and not (np.take_along_axis(k, k, axis=2) == PLACES).all(): b.append("pr: a place that isn't the pair of its pair")
        if ((d["wc"][r] == 0x7F) | (d["wc"][r] == 0xFF)).any(): b.append("wc: a code that is no number")
        s = mx_ref.live(d["ws"][r])
        if ((s != none) & ((s < least) | (s > most))).any(): b.append("ws: a scale out of range")
        if (((d["wc"][r].reshape(16, 8, 512, 4) & 0x7F) != 0) & (s == none)[:, None, :, None]).any(): b.append("wc: a code other than zero under the scale of zeros")
    return b
def at(a, e):
    return np.take_along_axis(a, e, axis=1)
def layer(w, q):
    return tile([mx_ref.matmul(pick(w, np.arange(128 * b, 128 * b + 128)), q) * np.float32(0.03125) for b in range(4)])
def reference(x, u, v, pp, rf, pr, wc, ws):
    qu = [mx_ref.quantize(u[r]) for r in range(N)]
    lay = [pk(wc[r], ws[r]) for r in range(N)]
    place, refs = [gentries(pp[r]) for r in range(N)], [gentries(rf[r]) for r in range(N)]
    pair = [gentries(pr[r]).reshape(8, 3, C) for r in range(N)]
    now = [x[r] for r in range(N)]
    for t, step in enumerate(STEP):
        held, mix = [], []
        for r in range(N):
            q = mx_ref.quantize(now[r])
            s = mx_ref.matmul(qu[r], q)
            sign, mode = s[::16] > 0, s[1::16] > 0
            held.append(decode(q))
            k, here = pair[r][:, t], at(sign, place[r])
            swap = np.where(here == at(here, k), k, PLACES)
            place[r] = at(place[r], swap)
            old = at(refs[r], swap)
            refs[r] = np.where(at(mode, place[r]), at(swap, old), (old + PLACES - swap) % C)
            g = held[r].astype(BF)
            z = gcols(g, place[r]).astype(np.float32) + gcols(g, at(place[r], refs[r])).astype(np.float32)
            mix.append(mx_ref.quantize((z * np.float32(0.5)).astype(BF)))
        for r in range(N):
            h = layer(lay[r], join(pick(mix[r], np.arange(H)), pick(mix[r ^ step], np.arange(H, C))))
            inverse = np.argsort(place[r], axis=1)
            now[r] = (held[r] + gcols(h, at(refs[r ^ step], at(refs[r], inverse))).astype(np.float32)).astype(BF)
    y, pf = np.zeros((N, 128, C), np.float32), np.zeros((N, 8, 2 * C), np.float32)
    oc, osc = np.zeros((N, 128, 4 * C), np.uint8), np.zeros((N, 16, C), np.uint8)
    for r in range(N):
        q = mx_ref.quantize(now[r])
        y[r] = mx_ref.matmul(mx_ref.quantize(v[r]), q)
        pf[r] = np.concatenate([place[r], refs[r]], axis=1)
        oc[r], osc[r] = emit(q)
    return {"y": y, "pf": pf, "oc": oc, "osc": osc}

@@ -1,0 +1,416 @@
+from concourse.bass import DstId, RemoteDMATransfer
+from concourse.mybir import dt, AluOpType, ActivationFunctionType
+
+C, H = 448, 224
+STEP = [1, 2, 3]
+ADD, SUB, MUL = AluOpType.add, AluOpType.subtract, AluOpType.mult
+GT, GE, LT, EQ, NE = AluOpType.is_gt, AluOpType.is_ge, AluOpType.is_lt, AluOpType.is_equal, AluOpType.not_equal
+COPY, SIGN = ActivationFunctionType.Copy, ActivationFunctionType.Sign
+K = 16384.0
+KF = 32.0
+CODES = "float8_e4m3fn_x4"
+
+SCRATCH = {
+    "xin": ("sbuf", [128, 4 * C], "bfloat16"), "xt": ("sbuf", [128, 4 * C], "bfloat16"), "zt": ("sbuf", [128, 4 * C], "bfloat16"),
+    "ut": ("sbuf", [128, 512], "bfloat16"), "vt": ("sbuf", [128, 512], "bfloat16"), "ee": ("sbuf", [128, 2048], "bfloat16"),
+    "qx": ("sbuf", [128, C], CODES), "sx": ("sbuf", [128, C], "uint8"),
+    "qu": ("sbuf", [128, 128], CODES), "su": ("sbuf", [128, 128], "uint8"),
+    "qus": ("sbuf", [128, 256], CODES), "sus": ("sbuf", [128, 256], "uint8"),
+    "qv": ("sbuf", [128, 128], CODES), "sv": ("sbuf", [128, 128], "uint8"),
+    "qe": ("sbuf", [128, 512], CODES), "se": ("sbuf", [128, 512], "uint8"),
+    "qw": ("sbuf", [128, 512], CODES), "sw": ("sbuf", [128, 512], "uint8"),
+    "fp": ("sbuf", [128, 4 * C], "bfloat16"), "gp": ("sbuf", [128, 4 * C], "bfloat16"), "bp": ("sbuf", [128, 4 * C], "bfloat16"), "g2": ("sbuf", [128, 4 * C], "bfloat16"),
+    "tmp": ("sbuf", [128, 2 * C], "bfloat16"), "ysb": ("sbuf", [128, C], "float32"),
+    "ip": ("sbuf", [128, 1], "int32"), "ri": ("sbuf", [128, 1], "int32"), "cc": ("sbuf", [128, 8], "float32"),
+    "iot": ("sbuf", [128, 512], "float32"), "dj": ("sbuf", [128, 16], "float32"), "c1": ("sbuf", [128, 16], "float32"),
+    "c2": ("sbuf", [128, 32], "float32"), "c16": ("sbuf", [128, 32], "float32"), "roff": ("sbuf", [128, 28], "uint16"),
+    "cf": ("sbuf", [128, C], "float32"), "cb": ("sbuf", [128, C], "bfloat16"),
+    "uoi": ("sbuf", [128, 16], "int32"), "uoff": ("sbuf", [128, 16], "uint16"),
+    "ppi": ("sbuf", [128, 28], "int32"), "rfi": ("sbuf", [128, 28], "int32"), "pri": ("sbuf", [128, 84], "int32"),
+    "qo": ("sbuf", [128, 28], "float32"), "ku": ("sbuf", [128, 84], "uint16"), "pfo": ("sbuf", [128, 56], "float32"),
+    "nqk": ("sbuf", [128, 84], "float32"), "pkfk": ("sbuf", [128, 56], "float32"), "pku": ("sbuf", [128, 28], "uint16"),
+    "xa": ("sbuf", [128, 28], "float32"), "w1": ("sbuf", [128, 28], "float32"), "w2": ("sbuf", [128, 28], "float32"),
+    "xb": ("sbuf", [128, 28], "float32"), "xc": ("sbuf", [128, 28], "float32"),
+    "d0": ("sbuf", [128, 224], "float32"), "do": ("sbuf", [128, 224], "float32"),
+    "s30": ("sbuf", [128, 84], "float32"), "s31": ("sbuf", [128, 84], "float32"), "s3o": ("sbuf", [128, 84], "float32"),
+    "sa": ("sbuf", [128, C], "bfloat16"), "bs": ("sbuf", [128, C], "bfloat16"),
+    "h1": ("sbuf", [128, C], "bfloat16"), "h2": ("sbuf", [128, C], "bfloat16"), "hb": ("sbuf", [128, C], "bfloat16"),
+    "hs": ("sbuf", [128, 2 * C], "bfloat16"), "hbs": ("sbuf", [128, C], "bfloat16"), "fl": ("sbuf", [128, 56], "float32"),
+    "cu": ("sbuf", [128, 28], "uint16"), "eu": ("sbuf", [128, 28], "uint16"),
+    "tw": ("sbuf", [128, C], "float32"), "tcw": ("sbuf", [128, C], "float32"), "tcs": ("sbuf", [128, C], "float32"),
+    "inw": ("sbuf", [128, C], "float32"), "ins": ("sbuf", [128, C], "float32"),
+    "pw": ("sbuf", [128, C], "float32"), "fw": ("sbuf", [128, C], "float32"),
+    "pkw": ("sbuf", [128, C], "float32"), "fkw": ("sbuf", [128, C], "float32"), "pks": ("sbuf", [128, 2 * C], "float32"),
+    "fsw": ("sbuf", [128, C], "float32"), "c2w": ("sbuf", [128, C], "float32"), "ew": ("sbuf", [128, C], "float32"),
+    "es": ("sbuf", [128, C], "float32"),
+}
+for _t in range(3):
+    SCRATCH["d1%d" % _t] = ("sbuf", [128, 224], "float32")
+    SCRATCH["qzu%d" % _t] = ("sbuf", [128, H], CODES)
+    SCRATCH["szu%d" % _t] = ("sbuf", [128, H], "uint8")
+    SCRATCH["qy%d" % _t] = ("sbuf", [128, C], CODES)
+    SCRATCH["sy%d" % _t] = ("sbuf", [128, C], "uint8")
+    SCRATCH["fs%d" % _t] = ("sbuf", [128, 28], "uint16")
+for _t in range(4):
+    SCRATCH["lu%d" % _t] = ("sbuf", [128, 84], "uint16")
+    SCRATCH["inv%d" % _t] = ("sbuf", [128, 28], "uint16")
+for _t in range(8):
+    SCRATCH["ps%d" % _t] = ("psum", [128, 512], "float32")
+
+LOADS = ["pp", "rf", "pr", "u", "v", "x0", "x1", "wc", "ws", "g0", "g1", "g2", "g3"]
+SEMAPHORES = ["kv", "ks", "kt", "kg", "loc", "outy", "outs"] + ["l_" + n for n in LOADS] + \
+    ["fr%d" % t for t in range(3)] + ["zr%d" % t for t in range(3)]
+
+
+def rank_program(g, core, T, topo):
+    rank = T.rank_of(core)
+    if rank is None:
+        return
+    Q = {"v": g.vector, "s": g.scalar, "t": g.tensor, "g": g, "y": g.sync}
+    OWN = {"v": "kv", "s": "ks", "t": "kt", "g": "kg"}
+    known = {q: {} for q in Q}
+    total = {}
+    waited = {}
+    recs = {}
+
+    def wait(q, sem, val, clk):
+        Q[q].wait_ge(T.sem[sem], val)
+        waited[sem] = max(waited.get(sem, 0), val)
+        for k in clk:
+            known[q][k] = max(known[q].get(k, 0), clk[k])
+
+    def need(q, R, W):
+        req = {}
+        for w, regs in ((False, R), (True, W)):
+            for b, lo, hi in regs:
+                excl = w or b[:2] == "ps"
+                for r in recs.get(b, []):
+                    if r[0] < hi and lo < r[1] and (r[5] or excl):
+                        if r[4] == q and not r[5]:
+                            continue
+                        if r[4] == q and b[:2] == "ps" and not w and not r[5]:
+                            continue
+                        sem, val = r[2]
+                        if known[q].get(sem, 0) < val and (sem not in req or req[sem][0] < val):
+                            req[sem] = (val, r[3])
+        for sem in sorted(req):
+            val, clk = req[sem]
+            if known[q].get(sem, 0) >= val:
+                continue
+            if any(o != sem and known[q].get(o, 0) < req[o][0] and req[o][1].get(sem, 0) >= val for o in req):
+                continue
+            wait(q, sem, val, clk)
+
+    def note(q, R, W, tok, clk):
+        for w, regs in ((False, R), (True, W)):
+            for b, lo, hi in regs:
+                l = recs.setdefault(b, [])
+                if w:
+                    l = [r for r in l if not (lo <= r[0] and r[1] <= hi)]
+                else:
+                    l = [r for r in l if not (r[4] == q and not r[5] and lo <= r[0] and r[1] <= hi)]
+                l.append((lo, hi, tok, clk, q, w))
+                recs[b] = l
+
+    def op(q, make, R, W):
+        need(q, R, W)
+        sem = OWN[q]
+        total[sem] = total.get(sem, 0) + 1
+        make().then_inc(T.sem[sem], 1)
+        clk = dict(known[q])
+        clk[sem] = total[sem]
+        note(q, R, W, (sem, total[sem]), clk)
+
+    def dma(q, out, in_, sem, R, W):
+        need(q, R, W)
+        total[sem] = total.get(sem, 0) + 16
+        Q[q].dma_start(out, in_).then_inc(T.sem[sem], 16)
+        clk = dict(known[q])
+        clk[sem] = total[sem]
+        note("d" + q, R, W, (sem, total[sem]), clk)
+
+    def landed(sem, val, W):
+        total[sem] = val
+        note("remote", [], W, (sem, val), {sem: val})
+
+    V, S = g.vector, g.scalar
+
+    def tab(n):
+        return (n, 0, C)
+
+    def ind(n, off, a=0, b=28, lo=0, hi=C):
+        return T[n][:, lo:hi].indirect(T[off][:, a:b])
+
+    def look(q, out, win, off, a=0, b=28, roff=None, rwin=None):
+        def make():
+            if q == "s":
+                return S.activation(T[out][:, :], ind(win, off, a, b), COPY)
+            return V.tensor_copy(T[out][:, :], ind(win, off, a, b))
+        op(q, make, [rwin or tab(win), roff or (off, a, b)], [tab(out)])
+
+    def scan(src, out, o=0, flags=False):
+        c = "cb" if flags else "cf"
+        op("v", lambda: V.tensor_tensor_scan(T[out][:, o:o + C], T[c][:, :], T[src][:, :], 0.0, MUL, ADD), [tab(src), tab(c)], [(out, o, o + C)])
+
+    dma("y", T.ppi[:, :], T.pp[:, :], "l_pp", [], [("ppi", 0, 28)])
+    dma("s", T.rfi[:, :], T.rf[:, :], "l_rf", [], [("rfi", 0, 28)])
+    dma("y", T.pri[:, :], T.pr[:, :], "l_pr", [], [("pri", 0, 84)])
+    dma("s", T.ut[:, :], T.u[:, :], "l_u", [], [("ut", 0, 512)])
+    dma("y", T.xin[:, 0:4 * H], T.x[:, 0:4 * H], "l_x0", [], [("xin", 0, 4 * H)])
+    dma("s", T.xin[:, 4 * H:4 * C], T.x[:, 4 * H:4 * C], "l_x1", [], [("xin", 4 * H, 4 * C)])
+    dma("y", T.qw[:, :].bitcast(dt.uint8), T.wc[:, :], "l_wc", [], [("qw", 0, 512)])
+    dma("y", T.sw[:, :], T.ws[:, :], "l_ws", [], [("sw", 0, 512)])
+    dma("y", T.vt[:, :], T.v[:, :], "l_v", [], [("vt", 0, 512)])
+
+    op("g", lambda: g.iota(T.ip[:, :], [[0, 1]], 0, 1), [], [("ip", 0, 1)])
+    op("g", lambda: g.iota(T.iot[:, :], [[1, 512]], 0, 0, allow_small_or_imprecise_dtypes=True), [], [("iot", 0, 512)])
+    op("g", lambda: g.iota(T.uoi[:, :], [[1, 2], [16, 8]], 0, 0), [], [("uoi", 0, 16)])
+    op("v", lambda: V.memset(T.d0[:, :], 0.0), [], [("d0", 0, 224)] + [("d0o%d" % i, 0, 28) for i in range(4)])
+    op("v", lambda: V.memset(T.s30[:, :], 0.0), [], [("s30", 0, 84), ("s30f", 0, 28)])
+
+    def ts(out, in0, s1, s2, o0, o1, R, W):
+        if o1 is None:
+            op("v", lambda: V.tensor_scalar(out, in0, s1, None, o0), R, W)
+        else:
+            op("v", lambda: V.tensor_scalar(out, in0, s1, s2, o0, o1), R, W)
+
+    def tt(out, a, b, o, R, W):
+        op("v", lambda: V.tensor_tensor(out, a, b, o), R, W)
+
+    def cp(out, a, R, W):
+        op("v", lambda: V.tensor_copy(out, a), R, W)
+
+    cc = T.cc
+    ts(T.ri[:, :], T.ip[:, :], 15, None, AluOpType.bitwise_and, None, [("ip", 0, 1)], [("ri", 0, 1)])
+    ts(cc[:, 1:2], T.ip[:, :], 4.0, None, MUL, None, [("ip", 0, 1)], [("cc", 1, 2)])
+    cp(cc[:, 0:1], T.ri[:, :], [("ri", 0, 1)], [("cc", 0, 1)])
+    Rr, Rio = ("cc", 0, 1), ("iot", 0, 512)
+    ts(T.dj[:, :], T.iot[:, 0:16], cc[:, 0:1], None, SUB, None, [Rr, Rio], [("dj", 0, 16)])
+    ts(T.roff[:, :], T.iot[:, 0:28], 0.0, cc[:, 0:1], MUL, ADD, [Rr, Rio], [("roff", 0, 28)])
+    ts(cc[:, 4:5], cc[:, 0:1], 14.5, 1.0 - 1.0 / K, GE, MUL, [Rr], [("cc", 4, 5)])
+    ts(cc[:, 5:6], cc[:, 0:1], 14.5, 0.5 - KF / 2, GE, MUL, [Rr], [("cc", 5, 6)])
+    ts(T.c1[:, :], T.dj[:, :], 0.0, None, NE, None, [("dj", 0, 16)], [("c1", 0, 16)])
+    ts(T.c2[:, 0:16], T.dj[:, :], 1.0, K - 1.0, EQ, MUL, [("dj", 0, 16)], [("c2", 0, 16)])
+    ts(T.c2[:, 16:32], T.dj[:, :], 1.0, KF - 1.0, EQ, MUL, [("dj", 0, 16)], [("c2", 16, 32)])
+    tt(T.c16[:, 0:16], T.c1[:, :], T.c2[:, 0:16], ADD, [("c1", 0, 16), ("c2", 0, 16)], [("c16", 0, 16)])
+    tt(T.c16[:, 16:32], T.c1[:, :], T.c2[:, 16:32], ADD, [("c1", 0, 16), ("c2", 16, 32)], [("c16", 16, 32)])
+    ts(cc[:, 2:3], cc[:, 4:5], 1.0 / K, None, ADD, None, [("cc", 4, 5)], [("cc", 2, 3)])
+    ts(cc[:, 3:4], cc[:, 5:6], KF / 2, None, ADD, None, [("cc", 5, 6)], [("cc", 3, 4)])
+    SK, RSK, TH, RTH = cc[:, 2:3], ("cc", 2, 3), cc[:, 3:4], ("cc", 3, 4)
+    ts(T.qo[:, :], T.iot[:, 0:28], 16.0, cc[:, 0:1], MUL, ADD, [Rr, Rio], [("qo", 0, 28)])
+    ts(T.s30[:, 1:84:3], T.iot[:, 0:28], 0.0, SK, MUL, ADD, [RSK, Rio, ], [("s30", 0, 84)])
+    cp(T.uoff[:, :], T.uoi[:, :], [("uoi", 0, 16)], [("uoff", 0, 16)])
+    op("s", lambda: S.activation(T.cf[:, :], T.c16[:, 0:16].indirect(T.roff[:, 0:28]), COPY), [("c16", 0, 16), ("roff", 0, 28)], [tab("cf")])
+    op("s", lambda: S.activation(T.cb[:, :], T.c16[:, 16:32].indirect(T.roff[:, 0:28]), COPY), [("c16", 16, 32), ("roff", 0, 28)], [tab("cb")])
+
+    cp(T.lu3[:, 28:56], T.ppi[:, :], [("ppi", 0, 28)], [("lu3", 28, 56)])
+    cp(T.lu3[:, 56:84], T.rfi[:, :], [("rfi", 0, 28)], [("lu3", 56, 84)])
+    cp(T.ku[:, :], T.pri[:, :], [("pri", 0, 84)], [("ku", 0, 84)])
+    iotw = ("iot", 0, 512)
+    look("s", "pw", "iot", "lu3", 28, 56, rwin=iotw)
+    look("s", "pkw", "pw", "ku", 0, 28)
+    look("s", "fw", "iot", "lu3", 56, 84, rwin=iotw)
+    look("s", "fkw", "fw", "ku", 0, 28)
+    for b in range(4):
+        ts(T.ee[:, 512 * b:512 * b + 512], T.iot[:, :], cc[:, 1:2], float(b), SUB, EQ, [("cc", 1, 2), iotw], [("ee", 512 * b, 512 * b + 512)])
+    op("v", lambda: V.quantize_mx(T.qe[:, :], T.se[:, :], T.ee[:, :]), [("ee", 0, 2048)], [("qe", 0, 512), ("se", 0, 512)])
+    op("v", lambda: V.quantize_mx(T.qu[:, :], T.su[:, :], T.ut[:, :]), [("ut", 0, 512)], [("qu", 0, 128), ("su", 0, 128)])
+    op("v", lambda: V.tensor_copy(T.qus[:, 0:256].bitcast(dt.uint32), T.qu[:, 0:128].bitcast(dt.uint32).indirect(T.uoff[:, 0:16])),
+       [("qu", 0, 128), ("uoff", 0, 16)], [("qus", 0, 256)])
+    op("v", lambda: V.tensor_copy(T.sus[:, 0:256], T.su[:, 0:128].indirect(T.uoff[:, 0:16])), [("su", 0, 128), ("uoff", 0, 16)], [("sus", 0, 256)])
+    for t in range(3):
+        k = T.pri[:, 28 * t:28 * t + 28]
+        tt(T["d1%d" % t][:, 0:56:2], k, T.qo[:, :], SUB, [("pri", 0, 84), ("qo", 0, 28)], [("d1d%d" % t, 0, 28)])
+        tt(T.nqk[:, 28 * t:28 * t + 28], T.qo[:, :], k, SUB, [("pri", 0, 84), ("qo", 0, 28)], [("nqk", 28 * t, 28 * t + 28)])
+        cp(T["d1%d" % t][:, 1:56:2], T.qo[:, :], [("qo", 0, 28)], [("d1b%d" % t, 0, 28)])
+    scan("pkw", "pks", 0)
+    op("v", lambda: V.tensor_copy(T.inw[:, 0:C].indirect(T.lu3[:, 28:56]), T.iot[:, 0:C]), [("lu3", 28, 56), iotw], [tab("inw")])
+    for h in range(2):
+        op("v", lambda: V.quantize_mx(T.qx[:, H * h:H * h + H], T.sx[:, H * h:H * h + H], T.xin[:, 4 * H * h:4 * H * h + 4 * H]),
+           [("xin", 4 * H * h, 4 * H * h + 4 * H)], [("qx", H * h, H * h + H), ("sx", H * h, H * h + H)])
+    scan("fkw", "pks", C)
+    scan("inw", "ins")
+    ts(T.inv3[:, :], T.ins[:, 15:C:16], SK, None, MUL, None, [tab("ins"), RSK], [("inv3", 0, 28)])
+
+    def prep(t, lu):
+        d1 = T["d1%d" % t]
+        ts(T.pku[:, :], T.pks[:, 15:C:16], SK, None, MUL, None, [("pks", 0, C), RSK], [("pku", 0, 28)])
+        ts(T.pkfk[:, :], T.pks[:, 15:2 * C:16], SK, None, MUL, None, [("pks", 0, 2 * C), RSK], [("pkfk", 0, 56)])
+        cp(T.pfo[:, :], T[lu][:, 28:84], [(lu, 28, 84)], [("pfo", 0, 56)])
+        tt(T.xa[:, :], T.pkfk[:, 28:56], T.nqk[:, 28 * t:28 * t + 28], ADD, [("pkfk", 0, 56), ("nqk", 28 * t, 28 * t + 28)], [("xa", 0, 28)])
+        tt(d1[:, 56:168:2], T.pkfk[:, :], T.pfo[:, :], SUB, [("pkfk", 0, 56), ("pfo", 0, 56)], [("d1d%d" % t, 28, 84)])
+        ts(T.w1[:, :], T.xa[:, :], -0.5, 448.0, LT, MUL, [("xa", 0, 28)], [("w1", 0, 28)])
+        ts(T.w2[:, :], T.xa[:, :], 447.5, -448.0, GE, MUL, [("xa", 0, 28)], [("w2", 0, 28)])
+        tt(T.xb[:, :], T.xa[:, :], T.pfo[:, 28:56], SUB, [("xa", 0, 28), ("pfo", 0, 56)], [("xb", 0, 28)])
+        tt(T.xc[:, :], T.w1[:, :], T.w2[:, :], ADD, [("w1", 0, 28), ("w2", 0, 28)], [("xc", 0, 28)])
+        cp(d1[:, 57:168:2], T.pfo[:, :], [("pfo", 0, 56)], [("d1b%d" % t, 28, 84)])
+        cp(d1[:, 169:224:2], T.pfo[:, 28:56], [("pfo", 0, 56)], [("d1b%d" % t, 84, 112)])
+        tt(d1[:, 168:224:2], T.xb[:, :], T.xc[:, :], ADD, [("xb", 0, 28), ("xc", 0, 28)], [("d1d%d" % t, 84, 112)])
+
+    def mm(bank, n, st, sts, a, mv, mvs, lo):
+        op("t", lambda: g.tensor.matmul_mx(T["ps%d" % bank][:, 0:n], T[st][:, a:a + 128], T[sts][:, a:a + 128], T[mv][:, lo:lo + n], T[mvs][:, lo:lo + n], True, True),
+           [(st, a, a + 128), (sts, a, a + 128), (mv, lo, lo + n), (mvs, lo, lo + n)], [("ps%d" % bank, 0, 512)])
+
+    FB = [4, 5, 0, 1]
+
+    def evac(q, bank, n, out, o, key, scale):
+        src = T["ps%d" % bank][:, 0:n]
+        dst = T[out][:, o:o + n]
+
+        def make():
+            if q == "s":
+                return S.activation(dst, src, COPY) if scale is None else S.activation(dst, src, COPY, scale=scale)
+            return V.tensor_copy(dst, src) if scale is None else V.tensor_scalar(dst, src, scale, None, MUL)
+        op(q, make, [("ps%d" % bank, 0, 512)], [key])
+
+    def gather_g(q, b, lu):
+        src = T.fp[:, C * b:C * b + C].indirect(T[lu][:, 28:56])
+        dst = T.gp[:, C * b:C * b + C]
+
+        def make():
+            if q == "s":
+                return S.activation(dst, src, COPY, scale=0.5)
+            return V.tensor_scalar(dst, src, 0.5, None, MUL)
+        op(q, make, [("fp", C * b, C * b + C), (lu, 28, 56)], [("gp", C * b, C * b + C)])
+        dma("y", T.g2[:, C * b:C * b + H], T.gp[:, C * b:C * b + H], "l_g%d" % b, [("gp", C * b, C * b + C)], [("g2", C * b, C * b + H)])
+
+    def addend(b):
+        cp(T.g2[:, C * b + H:C * b + C], T.gp[:, C * b + H:C * b + C], [("gp", C * b, C * b + C)], [("g2", C * b + H, C * b + C)])
+
+    for t in range(3):
+        last = t == 2
+        lp, lu = "lu%d" % ((t - 1) % 4), "lu%d" % t
+        ip_, in_ = "inv%d" % ((t - 1) % 4), "inv%d" % t
+        dst = T.cores[rank ^ STEP[t]]
+        rid, pid, _ = topo.addr(dst)
+        eng = topo.engines(core, dst)
+        d1 = T["d1%d" % t]
+        mm(2, C, "qus", "sus", 0, "qx", "sx", 0)
+        for b in range(4):
+            mm(FB[b], C, "qe", "se", 128 * b, "qx", "sx", 0)
+        mm(3, C, "qus", "sus", 128, "qx", "sx", 0)
+        prep(t, lp)
+        op("v", lambda: V.tensor_scalar(T.sa[:, :], T.ps2[:, 0:C], 0.0, None, GT), [("ps2", 0, 512)], [tab("sa")])
+        look("s", "h2", "sa", "pku")
+        look("v", "h1", "sa", lp, 28, 56)
+        scan("h1", "hs", 0, True)
+        scan("h2", "hs", C, True)
+        for b in range(3):
+            evac("s", FB[b], C, "fp", C * b, ("fp", C * b, C * b + C), None)
+        op("s", lambda: S.activation(T.bs[:, :], T.ps3[:, 0:C], SIGN), [("ps3", 0, 512)], [tab("bs")])
+        ts(T.fl[:, :], T.hs[:, 15:2 * C:16], TH, None, GE, None, [("hs", 0, 2 * C), RTH], [("fl", 0, 56)])
+        for i in range(4):
+            tt(T.d0[:, 56 * i + 1:56 * i + 56:2], T.fl[:, 0:28], T.fl[:, 28:56], EQ, [("fl", 0, 56)], [("d0o%d" % i, 0, 28)])
+        for i in (0, 1):
+            op("v", lambda: V.tensor_tensor_scan(T.do[:, 112 * i:112 * i + 112], T.d0[:, 112 * i:112 * i + 112], d1[:, 112 * i:112 * i + 112], 0.0, MUL, ADD),
+               [("d0", 0, 224), ("d0o%d" % (2 * i), 0, 28), ("d0o%d" % (2 * i + 1), 0, 28), ("d1d%d" % t, 56 * i, 56 * i + 56), ("d1b%d" % t, 56 * i, 56 * i + 56)],
+               [("do", 112 * i, 112 * i + 112)])
+        cp(T[lu][:, 0:56], T.do[:, 1:112:2], [("do", 0, 112)], [(lu, 0, 56)])
+        cp(T.cu[:, :], T.do[:, 113:168:2], [("do", 112, 224)], [("cu", 0, 28)])
+        look("s", "tw", "iot", lu, 0, 28, rwin=iotw)
+        look("s", "tcw", "tw", "cu")
+        look("s", "hb", "bs", lu, 28, 56)
+        evac("v", FB[3], C, "fp", C * 3, ("fp", C * 3, C * 4), None)
+        cp(T.s31[:, 2:84:3], T.do[:, 169:224:2], [("do", 112, 224)], [("s31c", 0, 28)])
+        ts(T.s31[:, 1:84:3], T.do[:, 169:224:2], -1.0, None, MUL, None, [("do", 112, 224)], [("s31b", 0, 28)])
+        gather_g("v", 0, lu)
+        gather_g("v", 1, lu)
+        addend(0)
+        scan("tcw", "tcs")
+        gather_g("v", 2, lu)
+        gather_g("s", 3, lu)
+        addend(1)
+        addend(2)
+        cp(T.s31[:, 0:84:3], T.tcs[:, 15:C:16], [tab("tcs")], [("s31a", 0, 28)])
+        scan("hb", "hbs", 0, True)
+        ts(T.s30[:, 2:84:3], T.hbs[:, 15:C:16], TH, None, GE, None, [tab("hbs"), RTH], [("s30f", 0, 28)])
+        op("v", lambda: V.tensor_tensor_scan(T.s3o[:, :], T.s30[:, :], T.s31[:, :], 0.0, MUL, ADD),
+           [("s30", 0, 84), ("s30f", 0, 28), ("s31a", 0, 28), ("s31b", 0, 28), ("s31c", 0, 28)], [("s3o", 0, 84)])
+        cp(T[lu][:, 56:84], T.s3o[:, 2:84:3], [("s3o", 0, 84)], [(lu, 56, 84)])
+        need("g", [(lu, 56, 84)], [])
+        fe = eng[0:8]
+        g.remote_dma(T["fs%d" % t][:, :], T[lu][:, 56:84], T.sem["fr%d" % t], T.sem.loc, pid, rid, sum(1 << e for e in fe))
+        total["loc"] = total.get("loc", 0) + len(fe)
+        landed("fr%d" % t, len(fe), [("fs%d" % t, 0, 28)])
+        for h in (1, 0):
+            if h:
+                addend(3)
+            for b in range(4):
+                src = T.gp[:, C * b:C * b + C].indirect(T[lu][:, 56 + 14 * h:70 + 14 * h])
+                tt(T.zt[:, 4 * H * h + b:4 * H * h + 4 * H:4], src, T.g2[:, C * b + H * h:C * b + H * h + H], ADD,
+                   [("gp", C * b, C * b + C), (lu, 56, 84), ("g2", C * b + H * h, C * b + H * h + H)], [("zt%d" % b, H * h, H * h + H)])
+            R = [("zt%d" % b, H * h, H * h + H) for b in range(4)]
+            if h:
+                qz, sz = "qzu%d" % t, "szu%d" % t
+                op("v", lambda: V.quantize_mx(T[qz][:, :], T[sz][:, :], T.zt[:, 4 * H:4 * C]), R, [(qz, 0, H), (sz, 0, H)])
+                need("g", [(qz, 0, H), (sz, 0, H)], [])
+                qy, sy = "qy%d" % t, "sy%d" % t
+                to = [DstId(rid=rid, pnc=pid)]
+                n = H // 4
+                tr = []
+                for i in range(4):
+                    tr.append((T[qz][:, n * i:n * i + n].bitcast(dt.uint8), T[qy][:, H + n * i:H + n * i + n].bitcast(dt.uint8)))
+                tr.append((T[sz][:, :], T[sy][:, H:C]))
+                g.remote_dma_fused([RemoteDMATransfer(dst_ids=to, dma_engine_mask=sum(1 << e for e in eng[2 * i:2 * i + 2]), remote_sem=T.sem["zr%d" % t], src=a, dst=b)
+                                    for i, (a, b) in enumerate(tr)], local_sem=T.sem.loc)
+                total["loc"] += 10
+                landed("zr%d" % t, 10, [(qy, H, C), (sy, H, C)])
+            else:
+                op("v", lambda: V.quantize_mx(T[qy][:, 0:H], T[sy][:, 0:H], T.zt[:, 0:4 * H]), R, [(qy, 0, H), (sy, 0, H)])
+        look("s", "inw", "tw", ip_)
+        look("s", "pw", "iot", lu, 28, 56, rwin=iotw)
+        look("s", "fw", "iot", lu, 56, 84, rwin=iotw)
+        scan("inw", "ins")
+        ts(T[in_][:, :], T.ins[:, 15:C:16], SK, None, MUL, None, [tab("ins"), RSK], [(in_, 0, 28)])
+        if not last:
+            look("s", "pkw", "pw", "ku", 28 * t + 28, 28 * t + 56)
+            look("s", "fkw", "fw", "ku", 28 * t + 28, 28 * t + 56)
+        else:
+            dma("y", T.pf[:, 0:C], T.pw[0:128:16, :], "outy", [tab("pw")], [])
+            dma("y", T.pf[:, C:2 * C], T.fw[0:128:16, :], "outy", [tab("fw")], [])
+        look("s", "fsw", "iot", "fs%d" % t, 0, 28, rwin=iotw)
+        look("s", "c2w", "fsw", lu, 56, 84)
+        for b in range(4):
+            mm(2 + b % 2, H, "qw", "sw", 128 * b, qy, sy, 0)
+            evac("v" if b % 2 == 0 else "s", 2 + b % 2, H, "bp", C * b, ("bp", C * b, C * b + H), 0.03125)
+        look("s", "ew", "c2w", in_)
+        if not last:
+            scan("pkw", "pks", 0)
+            scan("fkw", "pks", C)
+        else:
+            op("v", lambda: V.quantize_mx(T.qv[:, :], T.sv[:, :], T.vt[:, :]), [("vt", 0, 512)], [("qv", 0, 128), ("sv", 0, 128)])
+        scan("ew", "es")
+        ts(T.eu[:, :], T.es[:, 15:C:16], SK, None, MUL, None, [tab("es"), RSK], [("eu", 0, 28)])
+        for b in range(4):
+            mm(4 + b, H, "qw", "sw", 128 * b, qy, sy, H)
+            evac("v" if b % 2 == 0 else "s", 4 + b, H, "bp", C * b + H, ("bp", C * b + H, C * b + C), 0.03125)
+        parts = [(0, H), (H, C)] if last else [(0, C)]
+        for lo, hi in parts:
+            a, e = lo // 16, hi // 16
+            for b in (2, 3):
+                op("s", lambda: S.activation(T.tmp[:, C * (b - 2) + lo:C * (b - 2) + hi], T.bp[:, C * b:C * b + C].indirect(T.eu[:, a:e]), COPY),
+                   [("bp", C * b, C * b + C), ("eu", 0, 28)], [("tmp", C * (b - 2) + lo, C * (b - 2) + hi)])
+            for b in range(4):
+                dst_ = T.xt[:, 4 * lo + b:4 * hi:4]
+                if b < 2:
+                    tt(dst_, T.bp[:, C * b:C * b + C].indirect(T.eu[:, a:e]), T.fp[:, C * b + lo:C * b + hi], ADD,
+                       [("bp", C * b, C * b + C), ("eu", 0, 28), ("fp", C * b, C * b + C)], [("xt%d" % b, lo, hi)])
+                else:
+                    tt(dst_, T.tmp[:, C * (b - 2) + lo:C * (b - 2) + hi], T["ps%d" % FB[b]][:, lo:hi], ADD,
+                       [("tmp", C * (b - 2) + lo, C * (b - 2) + hi), ("ps%d" % FB[b], 0, 512)], [("xt%d" % b, lo, hi)])
+            op("v", lambda: V.quantize_mx(T.qx[:, lo:hi], T.sx[:, lo:hi], T.xt[:, 4 * lo:4 * hi]),
+               [("xt%d" % b, lo, hi) for b in range(4)], [("qx", lo, hi), ("sx", lo, hi)])
+            if last:
+                bank = 6 + lo // H
+                mm(bank, H, "qv", "sv", 0, "qx", "sx", lo)
+                dma("y", T.oc[:, 4 * lo:4 * hi], T.qx[:, lo:hi].bitcast(dt.uint8), "outy", [("qx", lo, hi)], [])
+                if hi == C:
+                    for i in range(4):
+                        dma("y", T.osc[4 * i:4 * i + 4, :], T.sx[32 * i:32 * i + 4, :], "outy", [("sx", 0, C)], [])
+        if last:
+            for h in range(2):
+                evac("s", 6 + h, H, "ysb", H * h, ("ysb", H * h, H * h + H), None)
+                dma("s", T.y[:, H * h:H * h + H], T.ysb[:, H * h:H * h + H], "outs", [("ysb", H * h, H * h + H)], [])
+    for sem in sorted(total):
+        if waited.get(sem, 0) < total[sem]:
+            g.wait_ge(T.sem[sem], total[sem])

@@ -19,10 +19,10 @@ SCRATCH = {
     "qv": ("sbuf", [128, 128], CODES), "sv": ("sbuf", [128, 128], "uint8"),
     "qe": ("sbuf", [128, 512], CODES), "se": ("sbuf", [128, 512], "uint8"),
     "qw": ("sbuf", [128, 512], CODES), "sw": ("sbuf", [128, 512], "uint8"),
-    "fp": ("sbuf", [128, 4 * C], "bfloat16"), "gp": ("sbuf", [128, 4 * C], "bfloat16"), "bp": ("sbuf", [128, 4 * C], "bfloat16"), "g2": ("sbuf", [128, 4 * C], "bfloat16"),
-    "tmp": ("sbuf", [128, 2 * C], "bfloat16"), "ysb": ("sbuf", [128, C], "float32"),
+    "fp": ("sbuf", [128, 4 * C], "bfloat16"), "gp": ("sbuf", [128, 4 * C], "bfloat16"), "bp": ("sbuf", [128, 4 * C], "bfloat16"),
+    "g2": ("sbuf", [128, 4 * C], "bfloat16"), "tmp": ("sbuf", [128, 2 * C], "bfloat16"), "ysb": ("sbuf", [128, C], "float32"),
     "ip": ("sbuf", [128, 1], "int32"), "ri": ("sbuf", [128, 1], "int32"), "cc": ("sbuf", [128, 8], "float32"),
-    "iot": ("sbuf", [128, 512], "float32"), "dj": ("sbuf", [128, 16], "float32"), "c1": ("sbuf", [128, 16], "float32"),
+    "iot": ("sbuf", [128, C], "float32"), "dj": ("sbuf", [128, 16], "float32"), "c1": ("sbuf", [128, 16], "float32"),
     "c2": ("sbuf", [128, 32], "float32"), "c16": ("sbuf", [128, 32], "float32"), "roff": ("sbuf", [128, 28], "uint16"),
     "cf": ("sbuf", [128, C], "float32"), "cb": ("sbuf", [128, C], "bfloat16"),
     "uoi": ("sbuf", [128, 16], "int32"), "uoff": ("sbuf", [128, 16], "uint16"),
@@ -41,8 +41,8 @@ SCRATCH = {
     "inw": ("sbuf", [128, C], "float32"), "ins": ("sbuf", [128, C], "float32"),
     "pw": ("sbuf", [128, C], "float32"), "fw": ("sbuf", [128, C], "float32"),
     "pkw": ("sbuf", [128, C], "float32"), "fkw": ("sbuf", [128, C], "float32"), "pks": ("sbuf", [128, 2 * C], "float32"),
-    "fsw": ("sbuf", [128, C], "float32"), "c2w": ("sbuf", [128, C], "float32"), "ew": ("sbuf", [128, C], "float32"),
-    "es": ("sbuf", [128, C], "float32"),
+    "fsw": ("sbuf", [128, C], "float32"), "c2w": ("sbuf", [128, C], "float32"),
+    "ew": ("sbuf", [128, C], "float32"), "es": ("sbuf", [128, C], "float32"),
 }
 for _t in range(3):
     SCRATCH["d1%d" % _t] = ("sbuf", [128, 224], "float32")
@@ -51,9 +51,9 @@ for _t in range(3):
     SCRATCH["qy%d" % _t] = ("sbuf", [128, C], CODES)
     SCRATCH["sy%d" % _t] = ("sbuf", [128, C], "uint8")
     SCRATCH["fs%d" % _t] = ("sbuf", [128, 28], "uint16")
+    SCRATCH["inv%d" % _t] = ("sbuf", [128, 28], "uint16")
 for _t in range(4):
     SCRATCH["lu%d" % _t] = ("sbuf", [128, 84], "uint16")
-    SCRATCH["inv%d" % _t] = ("sbuf", [128, 28], "uint16")
 for _t in range(8):
     SCRATCH["ps%d" % _t] = ("psum", [128, 512], "float32")
 
@@ -85,11 +85,7 @@ def rank_program(g, core, T, topo):
             for b, lo, hi in regs:
                 excl = w or b[:2] == "ps"
                 for r in recs.get(b, []):
-                    if r[0] < hi and lo < r[1] and (r[5] or excl):
-                        if r[4] == q and not r[5]:
-                            continue
-                        if r[4] == q and b[:2] == "ps" and not w and not r[5]:
-                            continue
+                    if r[0] < hi and lo < r[1] and (r[5] or excl) and not (r[4] == q and not r[5]):
                         sem, val = r[2]
                         if known[q].get(sem, 0) < val and (sem not in req or req[sem][0] < val):
                             req[sem] = (val, r[3])
@@ -138,35 +134,16 @@ def rank_program(g, core, T, topo):
     def tab(n):
         return (n, 0, C)
 
-    def ind(n, off, a=0, b=28, lo=0, hi=C):
-        return T[n][:, lo:hi].indirect(T[off][:, a:b])
+    def look(q, out, win, off, a=0, b=28):
+        src = T[win][:, 0:C].indirect(T[off][:, a:b])
 
-    def look(q, out, win, off, a=0, b=28, roff=None, rwin=None):
         def make():
-            if q == "s":
-                return S.activation(T[out][:, :], ind(win, off, a, b), COPY)
-            return V.tensor_copy(T[out][:, :], ind(win, off, a, b))
-        op(q, make, [rwin or tab(win), roff or (off, a, b)], [tab(out)])
+            return S.activation(T[out][:, :], src, COPY) if q == "s" else V.tensor_copy(T[out][:, :], src)
+        op(q, make, [tab(win), (off, a, b)], [tab(out)])
 
     def scan(src, out, o=0, flags=False):
         c = "cb" if flags else "cf"
         op("v", lambda: V.tensor_tensor_scan(T[out][:, o:o + C], T[c][:, :], T[src][:, :], 0.0, MUL, ADD), [tab(src), tab(c)], [(out, o, o + C)])
-
-    dma("y", T.ppi[:, :], T.pp[:, :], "l_pp", [], [("ppi", 0, 28)])
-    dma("s", T.rfi[:, :], T.rf[:, :], "l_rf", [], [("rfi", 0, 28)])
-    dma("y", T.pri[:, :], T.pr[:, :], "l_pr", [], [("pri", 0, 84)])
-    dma("s", T.ut[:, :], T.u[:, :], "l_u", [], [("ut", 0, 512)])
-    dma("y", T.xin[:, 0:4 * H], T.x[:, 0:4 * H], "l_x0", [], [("xin", 0, 4 * H)])
-    dma("s", T.xin[:, 4 * H:4 * C], T.x[:, 4 * H:4 * C], "l_x1", [], [("xin", 4 * H, 4 * C)])
-    dma("y", T.qw[:, :].bitcast(dt.uint8), T.wc[:, :], "l_wc", [], [("qw", 0, 512)])
-    dma("y", T.sw[:, :], T.ws[:, :], "l_ws", [], [("sw", 0, 512)])
-    dma("y", T.vt[:, :], T.v[:, :], "l_v", [], [("vt", 0, 512)])
-
-    op("g", lambda: g.iota(T.ip[:, :], [[0, 1]], 0, 1), [], [("ip", 0, 1)])
-    op("g", lambda: g.iota(T.iot[:, :], [[1, 512]], 0, 0, allow_small_or_imprecise_dtypes=True), [], [("iot", 0, 512)])
-    op("g", lambda: g.iota(T.uoi[:, :], [[1, 2], [16, 8]], 0, 0), [], [("uoi", 0, 16)])
-    op("v", lambda: V.memset(T.d0[:, :], 0.0), [], [("d0", 0, 224)] + [("d0o%d" % i, 0, 28) for i in range(4)])
-    op("v", lambda: V.memset(T.s30[:, :], 0.0), [], [("s30", 0, 84), ("s30f", 0, 28)])
 
     def ts(out, in0, s1, s2, o0, o1, R, W):
         if o1 is None:
@@ -180,11 +157,27 @@ def rank_program(g, core, T, topo):
     def cp(out, a, R, W):
         op("v", lambda: V.tensor_copy(out, a), R, W)
 
+    dma("y", T.ppi[:, :], T.pp[:, :], "l_pp", [], [("ppi", 0, 28)])
+    dma("s", T.pri[:, :], T.pr[:, :], "l_pr", [], [("pri", 0, 84)])
+    dma("y", T.xin[:, 0:4 * H], T.x[:, 0:4 * H], "l_x0", [], [("xin", 0, 4 * H)])
+    dma("s", T.ut[:, :], T.u[:, :], "l_u", [], [("ut", 0, 512)])
+    dma("y", T.xin[:, 4 * H:4 * C], T.x[:, 4 * H:4 * C], "l_x1", [], [("xin", 4 * H, 4 * C)])
+    dma("y", T.rfi[:, :], T.rf[:, :], "l_rf", [], [("rfi", 0, 28)])
+    dma("y", T.qw[:, :].bitcast(dt.uint8), T.wc[:, :], "l_wc", [], [("qw", 0, 512)])
+    dma("y", T.sw[:, :], T.ws[:, :], "l_ws", [], [("sw", 0, 512)])
+    dma("y", T.vt[:, :], T.v[:, :], "l_v", [], [("vt", 0, 512)])
+
+    op("g", lambda: g.iota(T.ip[:, :], [[0, 1]], 0, 1), [], [("ip", 0, 1)])
+    op("g", lambda: g.iota(T.iot[:, :], [[1, C]], 0, 0, allow_small_or_imprecise_dtypes=True), [], [tab("iot")])
+    op("g", lambda: g.iota(T.uoi[:, :], [[1, 2], [16, 8]], 0, 0), [], [("uoi", 0, 16)])
+    op("v", lambda: V.memset(T.ee[:, :], 0.0), [], [("ee", 0, 2048)])
+    op("v", lambda: V.memset(T.d0[:, :], 0.0), [], [("d0", 0, 224)] + [("d0o%d" % i, 0, 28) for i in range(4)])
+    op("v", lambda: V.memset(T.s30[:, :], 0.0), [], [("s30", 0, 84), ("s30f", 0, 28)])
     cc = T.cc
     ts(T.ri[:, :], T.ip[:, :], 15, None, AluOpType.bitwise_and, None, [("ip", 0, 1)], [("ri", 0, 1)])
-    ts(cc[:, 1:2], T.ip[:, :], 4.0, None, MUL, None, [("ip", 0, 1)], [("cc", 1, 2)])
+    cp(cc[:, 1:2], T.ip[:, :], [("ip", 0, 1)], [("cc", 1, 2)])
     cp(cc[:, 0:1], T.ri[:, :], [("ri", 0, 1)], [("cc", 0, 1)])
-    Rr, Rio = ("cc", 0, 1), ("iot", 0, 512)
+    Rr, Rio = ("cc", 0, 1), tab("iot")
     ts(T.dj[:, :], T.iot[:, 0:16], cc[:, 0:1], None, SUB, None, [Rr, Rio], [("dj", 0, 16)])
     ts(T.roff[:, :], T.iot[:, 0:28], 0.0, cc[:, 0:1], MUL, ADD, [Rr, Rio], [("roff", 0, 28)])
     ts(cc[:, 4:5], cc[:, 0:1], 14.5, 1.0 - 1.0 / K, GE, MUL, [Rr], [("cc", 4, 5)])
@@ -198,54 +191,61 @@ def rank_program(g, core, T, topo):
     ts(cc[:, 3:4], cc[:, 5:6], KF / 2, None, ADD, None, [("cc", 5, 6)], [("cc", 3, 4)])
     SK, RSK, TH, RTH = cc[:, 2:3], ("cc", 2, 3), cc[:, 3:4], ("cc", 3, 4)
     ts(T.qo[:, :], T.iot[:, 0:28], 16.0, cc[:, 0:1], MUL, ADD, [Rr, Rio], [("qo", 0, 28)])
-    ts(T.s30[:, 1:84:3], T.iot[:, 0:28], 0.0, SK, MUL, ADD, [RSK, Rio, ], [("s30", 0, 84)])
     cp(T.uoff[:, :], T.uoi[:, :], [("uoi", 0, 16)], [("uoff", 0, 16)])
-    op("s", lambda: S.activation(T.cf[:, :], T.c16[:, 0:16].indirect(T.roff[:, 0:28]), COPY), [("c16", 0, 16), ("roff", 0, 28)], [tab("cf")])
-    op("s", lambda: S.activation(T.cb[:, :], T.c16[:, 16:32].indirect(T.roff[:, 0:28]), COPY), [("c16", 16, 32), ("roff", 0, 28)], [tab("cb")])
 
     cp(T.lu3[:, 28:56], T.ppi[:, :], [("ppi", 0, 28)], [("lu3", 28, 56)])
-    cp(T.lu3[:, 56:84], T.rfi[:, :], [("rfi", 0, 28)], [("lu3", 56, 84)])
     cp(T.ku[:, :], T.pri[:, :], [("pri", 0, 84)], [("ku", 0, 84)])
-    iotw = ("iot", 0, 512)
-    look("s", "pw", "iot", "lu3", 28, 56, rwin=iotw)
-    look("s", "pkw", "pw", "ku", 0, 28)
-    look("s", "fw", "iot", "lu3", 56, 84, rwin=iotw)
-    look("s", "fkw", "fw", "ku", 0, 28)
+    look("s", "pw", "iot", "lu3", 28, 56)
     for b in range(4):
-        ts(T.ee[:, 512 * b:512 * b + 512], T.iot[:, :], cc[:, 1:2], float(b), SUB, EQ, [("cc", 1, 2), iotw], [("ee", 512 * b, 512 * b + 512)])
-    op("v", lambda: V.quantize_mx(T.qe[:, :], T.se[:, :], T.ee[:, :]), [("ee", 0, 2048)], [("qe", 0, 512), ("se", 0, 512)])
+        ts(T.ee[:, 512 * b + b:512 * b + 512:4], T.iot[:, 0:128], cc[:, 1:2], None, EQ, None, [("cc", 1, 2), tab("iot"), ("ee", 0, 2048)], [("ee%d" % b, 0, 128)])
     op("v", lambda: V.quantize_mx(T.qu[:, :], T.su[:, :], T.ut[:, :]), [("ut", 0, 512)], [("qu", 0, 128), ("su", 0, 128)])
     op("v", lambda: V.tensor_copy(T.qus[:, 0:256].bitcast(dt.uint32), T.qu[:, 0:128].bitcast(dt.uint32).indirect(T.uoff[:, 0:16])),
        [("qu", 0, 128), ("uoff", 0, 16)], [("qus", 0, 256)])
-    op("v", lambda: V.tensor_copy(T.sus[:, 0:256], T.su[:, 0:128].indirect(T.uoff[:, 0:16])), [("su", 0, 128), ("uoff", 0, 16)], [("sus", 0, 256)])
-    for t in range(3):
+    op("s", lambda: S.activation(T.sus[:, 0:256], T.su[:, 0:128].indirect(T.uoff[:, 0:16]), COPY), [("su", 0, 128), ("uoff", 0, 16)], [("sus", 0, 256)])
+    look("s", "pkw", "pw", "ku", 0, 28)
+    op("s", lambda: S.activation(T.cf[:, :], T.c16[:, 0:16].indirect(T.roff[:, 0:28]), COPY), [("c16", 0, 16), ("roff", 0, 28)], [tab("cf")])
+
+    def exchange(t):
         k = T.pri[:, 28 * t:28 * t + 28]
         tt(T["d1%d" % t][:, 0:56:2], k, T.qo[:, :], SUB, [("pri", 0, 84), ("qo", 0, 28)], [("d1d%d" % t, 0, 28)])
         tt(T.nqk[:, 28 * t:28 * t + 28], T.qo[:, :], k, SUB, [("pri", 0, 84), ("qo", 0, 28)], [("nqk", 28 * t, 28 * t + 28)])
         cp(T["d1%d" % t][:, 1:56:2], T.qo[:, :], [("qo", 0, 28)], [("d1b%d" % t, 0, 28)])
-    scan("pkw", "pks", 0)
-    op("v", lambda: V.tensor_copy(T.inw[:, 0:C].indirect(T.lu3[:, 28:56]), T.iot[:, 0:C]), [("lu3", 28, 56), iotw], [tab("inw")])
-    for h in range(2):
-        op("v", lambda: V.quantize_mx(T.qx[:, H * h:H * h + H], T.sx[:, H * h:H * h + H], T.xin[:, 4 * H * h:4 * H * h + 4 * H]),
-           [("xin", 4 * H * h, 4 * H * h + 4 * H)], [("qx", H * h, H * h + H), ("sx", H * h, H * h + H)])
-    scan("fkw", "pks", C)
-    scan("inw", "ins")
-    ts(T.inv3[:, :], T.ins[:, 15:C:16], SK, None, MUL, None, [tab("ins"), RSK], [("inv3", 0, 28)])
 
-    def prep(t, lu):
+    def prep_p(t, lu):
         d1 = T["d1%d" % t]
         ts(T.pku[:, :], T.pks[:, 15:C:16], SK, None, MUL, None, [("pks", 0, C), RSK], [("pku", 0, 28)])
-        ts(T.pkfk[:, :], T.pks[:, 15:2 * C:16], SK, None, MUL, None, [("pks", 0, 2 * C), RSK], [("pkfk", 0, 56)])
-        cp(T.pfo[:, :], T[lu][:, 28:84], [(lu, 28, 84)], [("pfo", 0, 56)])
-        tt(T.xa[:, :], T.pkfk[:, 28:56], T.nqk[:, 28 * t:28 * t + 28], ADD, [("pkfk", 0, 56), ("nqk", 28 * t, 28 * t + 28)], [("xa", 0, 28)])
-        tt(d1[:, 56:168:2], T.pkfk[:, :], T.pfo[:, :], SUB, [("pkfk", 0, 56), ("pfo", 0, 56)], [("d1d%d" % t, 28, 84)])
+        ts(T.pkfk[:, 0:28], T.pks[:, 15:C:16], SK, None, MUL, None, [("pks", 0, C), RSK], [("pkfk", 0, 28)])
+        cp(T.pfo[:, 0:28], T[lu][:, 28:56], [(lu, 28, 56)], [("pfo", 0, 28)])
+        exchange(t)
+        tt(d1[:, 56:112:2], T.pkfk[:, 0:28], T.pfo[:, 0:28], SUB, [("pkfk", 0, 28), ("pfo", 0, 28)], [("d1d%d" % t, 28, 56)])
+        cp(d1[:, 57:112:2], T.pfo[:, 0:28], [("pfo", 0, 28)], [("d1b%d" % t, 28, 56)])
+
+    def prep_f(t, lu):
+        d1 = T["d1%d" % t]
+        cp(T.pfo[:, 28:56], T[lu][:, 56:84], [(lu, 56, 84)], [("pfo", 28, 56)])
+        ts(T.pkfk[:, 28:56], T.pks[:, C + 15:2 * C:16], SK, None, MUL, None, [("pks", C, 2 * C), RSK], [("pkfk", 28, 56)])
+        yield
+        cp(d1[:, 113:168:2], T.pfo[:, 28:56], [("pfo", 28, 56)], [("d1b%d" % t, 56, 84)])
+        tt(T.xa[:, :], T.pkfk[:, 28:56], T.nqk[:, 28 * t:28 * t + 28], ADD, [("pkfk", 28, 56), ("nqk", 28 * t, 28 * t + 28)], [("xa", 0, 28)])
+        tt(d1[:, 112:168:2], T.pkfk[:, 28:56], T.pfo[:, 28:56], SUB, [("pkfk", 28, 56), ("pfo", 28, 56)], [("d1d%d" % t, 56, 84)])
+        yield
         ts(T.w1[:, :], T.xa[:, :], -0.5, 448.0, LT, MUL, [("xa", 0, 28)], [("w1", 0, 28)])
         ts(T.w2[:, :], T.xa[:, :], 447.5, -448.0, GE, MUL, [("xa", 0, 28)], [("w2", 0, 28)])
-        tt(T.xb[:, :], T.xa[:, :], T.pfo[:, 28:56], SUB, [("xa", 0, 28), ("pfo", 0, 56)], [("xb", 0, 28)])
+        yield
+        tt(T.xb[:, :], T.xa[:, :], T.pfo[:, 28:56], SUB, [("xa", 0, 28), ("pfo", 28, 56)], [("xb", 0, 28)])
         tt(T.xc[:, :], T.w1[:, :], T.w2[:, :], ADD, [("w1", 0, 28), ("w2", 0, 28)], [("xc", 0, 28)])
-        cp(d1[:, 57:168:2], T.pfo[:, :], [("pfo", 0, 56)], [("d1b%d" % t, 28, 84)])
-        cp(d1[:, 169:224:2], T.pfo[:, 28:56], [("pfo", 0, 56)], [("d1b%d" % t, 84, 112)])
+        cp(d1[:, 169:224:2], T.pfo[:, 28:56], [("pfo", 28, 56)], [("d1b%d" % t, 84, 112)])
+        yield
         tt(d1[:, 168:224:2], T.xb[:, :], T.xc[:, :], ADD, [("xb", 0, 28), ("xc", 0, 28)], [("d1d%d" % t, 84, 112)])
+        yield
+
+    op("v", lambda: V.quantize_mx(T.qx[:, 0:H], T.sx[:, 0:H], T.xin[:, 0:4 * H]), [("xin", 0, 4 * H)], [("qx", 0, H), ("sx", 0, H)])
+    op("v", lambda: V.quantize_mx(T.qx[:, H:C], T.sx[:, H:C], T.xin[:, 4 * H:4 * C]), [("xin", 4 * H, 4 * C)], [("qx", H, C), ("sx", H, C)])
+    op("v", lambda: V.quantize_mx(T.qe[:, :], T.se[:, :], T.ee[:, :]), [("ee", 0, 2048)] + [("ee%d" % b, 0, 128) for b in range(4)], [("qe", 0, 512), ("se", 0, 512)])
+    scan("pkw", "pks", 0)
+    prep_p(0, "lu3")
+    cp(T.lu3[:, 56:84], T.rfi[:, :], [("rfi", 0, 28)], [("lu3", 56, 84)])
+    ts(T.s30[:, 1:84:3], T.iot[:, 0:28], 0.0, SK, MUL, ADD, [RSK, Rio, ], [("s30", 0, 84)])
 
     def mm(bank, n, st, sts, a, mv, mvs, lo):
         op("t", lambda: g.tensor.matmul_mx(T["ps%d" % bank][:, 0:n], T[st][:, a:a + 128], T[sts][:, a:a + 128], T[mv][:, lo:lo + n], T[mvs][:, lo:lo + n], True, True),
@@ -275,54 +275,82 @@ def rank_program(g, core, T, topo):
         dma("y", T.g2[:, C * b:C * b + H], T.gp[:, C * b:C * b + H], "l_g%d" % b, [("gp", C * b, C * b + C)], [("g2", C * b, C * b + H)])
 
     def addend(b):
-        cp(T.g2[:, C * b + H:C * b + C], T.gp[:, C * b + H:C * b + C], [("gp", C * b, C * b + C)], [("g2", C * b + H, C * b + C)])
+        d, s = T.g2[:, C * b + H:C * b + C], T.gp[:, C * b + H:C * b + C]
+        R, W = [("gp", C * b, C * b + C)], [("g2", C * b + H, C * b + C)]
+        if b < 2:
+            op("g", lambda: g.affine_select(d, s, [[0, H]], GT, 0.0, 1, 0), R, W)
+        else:
+            cp(d, s, R, W)
 
     for t in range(3):
         last = t == 2
         lp, lu = "lu%d" % ((t - 1) % 4), "lu%d" % t
-        ip_, in_ = "inv%d" % ((t - 1) % 4), "inv%d" % t
+        ip_, in_ = "inv%d" % ((t - 1) % 3), "inv%d" % t
         dst = T.cores[rank ^ STEP[t]]
         rid, pid, _ = topo.addr(dst)
         eng = topo.engines(core, dst)
         d1 = T["d1%d" % t]
-        mm(2, C, "qus", "sus", 0, "qx", "sx", 0)
+        for h in range(2):
+            mm(2 + h, H, "qus", "sus", 0, "qx", "sx", H * h)
         for b in range(4):
             mm(FB[b], C, "qe", "se", 128 * b, "qx", "sx", 0)
-        mm(3, C, "qus", "sus", 128, "qx", "sx", 0)
-        prep(t, lp)
-        op("v", lambda: V.tensor_scalar(T.sa[:, :], T.ps2[:, 0:C], 0.0, None, GT), [("ps2", 0, 512)], [tab("sa")])
+        mm(6, C, "qus", "sus", 128, "qx", "sx", 0)
+        for h in range(2):
+            op("s", lambda: S.activation(T.sa[:, H * h:H * h + H], T["ps%d" % (2 + h)][:, 0:H], SIGN), [("ps%d" % (2 + h), 0, 512)], [("sa", H * h, H * h + H)])
+        if t == 0:
+            op("s", lambda: S.activation(T.cb[:, :], T.c16[:, 16:32].indirect(T.roff[:, 0:28]), COPY), [("c16", 16, 32), ("roff", 0, 28)], [tab("cb")])
         look("s", "h2", "sa", "pku")
+        if t == 0:
+            look("s", "fw", "iot", "lu3", 56, 84)
+            look("s", "fkw", "fw", "ku", 0, 28)
+        else:
+            scan("fkw", "pks", C)
+        rest = prep_f(t, lp)
         look("v", "h1", "sa", lp, 28, 56)
+        if t > 0:
+            next(rest)
         scan("h1", "hs", 0, True)
         scan("h2", "hs", C, True)
+        if t > 0:
+            next(rest)
         for b in range(3):
             evac("s", FB[b], C, "fp", C * b, ("fp", C * b, C * b + C), None)
-        op("s", lambda: S.activation(T.bs[:, :], T.ps3[:, 0:C], SIGN), [("ps3", 0, 512)], [tab("bs")])
+        op("s", lambda: S.activation(T.bs[:, :], T.ps6[:, 0:C], SIGN), [("ps6", 0, 512)], [tab("bs")])
         ts(T.fl[:, :], T.hs[:, 15:2 * C:16], TH, None, GE, None, [("hs", 0, 2 * C), RTH], [("fl", 0, 56)])
+        if t > 0:
+            next(rest)
         for i in range(4):
             tt(T.d0[:, 56 * i + 1:56 * i + 56:2], T.fl[:, 0:28], T.fl[:, 28:56], EQ, [("fl", 0, 56)], [("d0o%d" % i, 0, 28)])
-        for i in (0, 1):
+
+        def select(i):
             op("v", lambda: V.tensor_tensor_scan(T.do[:, 112 * i:112 * i + 112], T.d0[:, 112 * i:112 * i + 112], d1[:, 112 * i:112 * i + 112], 0.0, MUL, ADD),
                [("d0", 0, 224), ("d0o%d" % (2 * i), 0, 28), ("d0o%d" % (2 * i + 1), 0, 28), ("d1d%d" % t, 56 * i, 56 * i + 56), ("d1b%d" % t, 56 * i, 56 * i + 56)],
                [("do", 112 * i, 112 * i + 112)])
+        select(0)
+        if t > 0:
+            next(rest)
         cp(T[lu][:, 0:56], T.do[:, 1:112:2], [("do", 0, 112)], [(lu, 0, 56)])
+        if t == 0:
+            scan("fkw", "pks", C)
+        for _i in rest:
+            pass
+        select(1)
+        evac("v", FB[3], C, "fp", C * 3, ("fp", C * 3, C * 4), None)
         cp(T.cu[:, :], T.do[:, 113:168:2], [("do", 112, 224)], [("cu", 0, 28)])
-        look("s", "tw", "iot", lu, 0, 28, rwin=iotw)
+        look("s", "tw", "iot", lu, 0, 28)
         look("s", "tcw", "tw", "cu")
         look("s", "hb", "bs", lu, 28, 56)
-        evac("v", FB[3], C, "fp", C * 3, ("fp", C * 3, C * 4), None)
+        gather_g("v", 0, lu)
         cp(T.s31[:, 2:84:3], T.do[:, 169:224:2], [("do", 112, 224)], [("s31c", 0, 28)])
         ts(T.s31[:, 1:84:3], T.do[:, 169:224:2], -1.0, None, MUL, None, [("do", 112, 224)], [("s31b", 0, 28)])
-        gather_g("v", 0, lu)
         gather_g("v", 1, lu)
         addend(0)
-        scan("tcw", "tcs")
-        gather_g("v", 2, lu)
-        gather_g("s", 3, lu)
         addend(1)
-        addend(2)
-        cp(T.s31[:, 0:84:3], T.tcs[:, 15:C:16], [tab("tcs")], [("s31a", 0, 28)])
+        gather_g("s", 2, lu)
+        gather_g("s", 3, lu)
+        scan("tcw", "tcs")
         scan("hb", "hbs", 0, True)
+        cp(T.s31[:, 0:84:3], T.tcs[:, 15:C:16], [tab("tcs")], [("s31a", 0, 28)])
         ts(T.s30[:, 2:84:3], T.hbs[:, 15:C:16], TH, None, GE, None, [tab("hbs"), RTH], [("s30f", 0, 28)])
         op("v", lambda: V.tensor_tensor_scan(T.s3o[:, :], T.s30[:, :], T.s31[:, :], 0.0, MUL, ADD),
            [("s30", 0, 84), ("s30f", 0, 28), ("s31a", 0, 28), ("s31b", 0, 28), ("s31c", 0, 28)], [("s3o", 0, 84)])
@@ -332,19 +360,19 @@ def rank_program(g, core, T, topo):
         g.remote_dma(T["fs%d" % t][:, :], T[lu][:, 56:84], T.sem["fr%d" % t], T.sem.loc, pid, rid, sum(1 << e for e in fe))
         total["loc"] = total.get("loc", 0) + len(fe)
         landed("fr%d" % t, len(fe), [("fs%d" % t, 0, 28)])
+        qz, sz, qy, sy = "qzu%d" % t, "szu%d" % t, "qy%d" % t, "sy%d" % t
+        addend(2)
         for h in (1, 0):
-            if h:
-                addend(3)
             for b in range(4):
                 src = T.gp[:, C * b:C * b + C].indirect(T[lu][:, 56 + 14 * h:70 + 14 * h])
                 tt(T.zt[:, 4 * H * h + b:4 * H * h + 4 * H:4], src, T.g2[:, C * b + H * h:C * b + H * h + H], ADD,
                    [("gp", C * b, C * b + C), (lu, 56, 84), ("g2", C * b + H * h, C * b + H * h + H)], [("zt%d" % b, H * h, H * h + H)])
+                if h and b == 1:
+                    addend(3)
             R = [("zt%d" % b, H * h, H * h + H) for b in range(4)]
             if h:
-                qz, sz = "qzu%d" % t, "szu%d" % t
                 op("v", lambda: V.quantize_mx(T[qz][:, :], T[sz][:, :], T.zt[:, 4 * H:4 * C]), R, [(qz, 0, H), (sz, 0, H)])
                 need("g", [(qz, 0, H), (sz, 0, H)], [])
-                qy, sy = "qy%d" % t, "sy%d" % t
                 to = [DstId(rid=rid, pnc=pid)]
                 n = H // 4
                 tr = []
@@ -357,39 +385,43 @@ def rank_program(g, core, T, topo):
                 landed("zr%d" % t, 10, [(qy, H, C), (sy, H, C)])
             else:
                 op("v", lambda: V.quantize_mx(T[qy][:, 0:H], T[sy][:, 0:H], T.zt[:, 0:4 * H]), R, [(qy, 0, H), (sy, 0, H)])
-        look("s", "inw", "tw", ip_)
-        look("s", "pw", "iot", lu, 28, 56, rwin=iotw)
-        look("s", "fw", "iot", lu, 56, 84, rwin=iotw)
-        scan("inw", "ins")
-        ts(T[in_][:, :], T.ins[:, 15:C:16], SK, None, MUL, None, [tab("ins"), RSK], [(in_, 0, 28)])
+        if t == 0:
+            op("v", lambda: V.tensor_copy(T.inw[:, 0:C].indirect(T[lu][:, 28:56]), T.iot[:, 0:C]), [(lu, 28, 56), tab("iot")], [tab("inw")])
+        else:
+            look("s", "inw", "tw", ip_)
+        look("s", "pw", "iot", lu, 28, 56)
         if not last:
             look("s", "pkw", "pw", "ku", 28 * t + 28, 28 * t + 56)
-            look("s", "fkw", "fw", "ku", 28 * t + 28, 28 * t + 56)
-        else:
-            dma("y", T.pf[:, 0:C], T.pw[0:128:16, :], "outy", [tab("pw")], [])
-            dma("y", T.pf[:, C:2 * C], T.fw[0:128:16, :], "outy", [tab("fw")], [])
-        look("s", "fsw", "iot", "fs%d" % t, 0, 28, rwin=iotw)
+        scan("inw", "ins")
+        ts(T[in_][:, :], T.ins[:, 15:C:16], SK, None, MUL, None, [tab("ins"), RSK], [(in_, 0, 28)])
+        look("s", "fsw", "iot", "fs%d" % t, 0, 28)
         look("s", "c2w", "fsw", lu, 56, 84)
         for b in range(4):
             mm(2 + b % 2, H, "qw", "sw", 128 * b, qy, sy, 0)
-            evac("v" if b % 2 == 0 else "s", 2 + b % 2, H, "bp", C * b, ("bp", C * b, C * b + H), 0.03125)
-        look("s", "ew", "c2w", in_)
+            if b == 2:
+                look("s", "ew", "c2w", in_)
+            evac("v" if last or (t == 0 and b % 2 == 1) else "s", 2 + b % 2, H, "bp", C * b, ("bp", C * b, C * b + H), 0.03125)
         if not last:
             scan("pkw", "pks", 0)
-            scan("fkw", "pks", C)
+            prep_p(t + 1, lu)
         else:
+            look("s", "fw", "iot", lu, 56, 84)
+            dma("y", T.pf[:, 0:C], T.pw[0:128:16, :], "outy", [tab("pw")], [])
+            dma("y", T.pf[:, C:2 * C], T.fw[0:128:16, :], "outy", [tab("fw")], [])
             op("v", lambda: V.quantize_mx(T.qv[:, :], T.sv[:, :], T.vt[:, :]), [("vt", 0, 512)], [("qv", 0, 128), ("sv", 0, 128)])
         scan("ew", "es")
         ts(T.eu[:, :], T.es[:, 15:C:16], SK, None, MUL, None, [tab("es"), RSK], [("eu", 0, 28)])
         for b in range(4):
             mm(4 + b, H, "qw", "sw", 128 * b, qy, sy, H)
             evac("v" if b % 2 == 0 else "s", 4 + b, H, "bp", C * b + H, ("bp", C * b + H, C * b + C), 0.03125)
-        parts = [(0, H), (H, C)] if last else [(0, C)]
-        for lo, hi in parts:
+        for lo, hi in ([(0, H), (H, C)] if last else [(0, C)]):
             a, e = lo // 16, hi // 16
             for b in (2, 3):
                 op("s", lambda: S.activation(T.tmp[:, C * (b - 2) + lo:C * (b - 2) + hi], T.bp[:, C * b:C * b + C].indirect(T.eu[:, a:e]), COPY),
                    [("bp", C * b, C * b + C), ("eu", 0, 28)], [("tmp", C * (b - 2) + lo, C * (b - 2) + hi)])
+            if not last:
+                look("s", "fw", "iot", lu, 56, 84)
+                look("s", "fkw", "fw", "ku", 28 * t + 28, 28 * t + 56)
             for b in range(4):
                 dst_ = T.xt[:, 4 * lo + b:4 * hi:4]
                 if b < 2:
@@ -398,11 +430,11 @@ def rank_program(g, core, T, topo):
                 else:
                     tt(dst_, T.tmp[:, C * (b - 2) + lo:C * (b - 2) + hi], T["ps%d" % FB[b]][:, lo:hi], ADD,
                        [("tmp", C * (b - 2) + lo, C * (b - 2) + hi), ("ps%d" % FB[b], 0, 512)], [("xt%d" % b, lo, hi)])
-            op("v", lambda: V.quantize_mx(T.qx[:, lo:hi], T.sx[:, lo:hi], T.xt[:, 4 * lo:4 * hi]),
-               [("xt%d" % b, lo, hi) for b in range(4)], [("qx", lo, hi), ("sx", lo, hi)])
+            for i in range(lo, hi, H):
+                op("v", lambda: V.quantize_mx(T.qx[:, i:i + H], T.sx[:, i:i + H], T.xt[:, 4 * i:4 * i + 4 * H]),
+                   [("xt%d" % b, lo, hi) for b in range(4)], [("qx", i, i + H), ("sx", i, i + H)])
             if last:
-                bank = 6 + lo // H
-                mm(bank, H, "qv", "sv", 0, "qx", "sx", lo)
+                mm(6 + lo // H, H, "qv", "sv", 0, "qx", "sx", lo)
                 dma("y", T.oc[:, 4 * lo:4 * hi], T.qx[:, lo:hi].bitcast(dt.uint8), "outy", [("qx", lo, hi)], [])
                 if hi == C:
                     for i in range(4):

@@ -2,6 +2,7 @@ from concourse.bass import DstId, RemoteDMATransfer
 from concourse.mybir import dt, AluOpType, ActivationFunctionType
 
 C, H = 448, 224
+CUT = 320
 STEP = [1, 2, 3]
 ADD, SUB, MUL = AluOpType.add, AluOpType.subtract, AluOpType.mult
 GT, GE, LT, EQ, NE = AluOpType.is_gt, AluOpType.is_ge, AluOpType.is_lt, AluOpType.is_equal, AluOpType.not_equal
@@ -22,12 +23,12 @@ SCRATCH = {
     "fp": ("sbuf", [128, 4 * C], "bfloat16"), "gp": ("sbuf", [128, 4 * C], "bfloat16"), "bp": ("sbuf", [128, 4 * C], "bfloat16"),
     "g2": ("sbuf", [128, 4 * C], "bfloat16"), "tmp": ("sbuf", [128, 2 * C], "bfloat16"), "ysb": ("sbuf", [128, C], "float32"),
     "ip": ("sbuf", [128, 1], "int32"), "ri": ("sbuf", [128, 1], "int32"), "cc": ("sbuf", [128, 8], "float32"),
-    "iot": ("sbuf", [128, C], "float32"), "dj": ("sbuf", [128, 16], "float32"), "c1": ("sbuf", [128, 16], "float32"),
-    "c2": ("sbuf", [128, 32], "float32"), "c16": ("sbuf", [128, 32], "float32"), "roff": ("sbuf", [128, 28], "uint16"),
-    "cf": ("sbuf", [128, C], "float32"), "cb": ("sbuf", [128, C], "bfloat16"),
+    "i28": ("sbuf", [128, 28], "float32"), "iot": ("sbuf", [128, C], "float32"), "dj": ("sbuf", [128, 16], "float32"),
+    "c1": ("sbuf", [128, 16], "float32"), "c2": ("sbuf", [128, 32], "float32"), "c16": ("sbuf", [128, 32], "float32"),
+    "roff": ("sbuf", [128, 28], "uint16"), "cf": ("sbuf", [128, C], "float32"), "cb": ("sbuf", [128, C], "bfloat16"),
     "uoi": ("sbuf", [128, 16], "int32"), "uoff": ("sbuf", [128, 16], "uint16"),
     "ppi": ("sbuf", [128, 28], "int32"), "rfi": ("sbuf", [128, 28], "int32"), "pri": ("sbuf", [128, 84], "int32"),
-    "qo": ("sbuf", [128, 28], "float32"), "ku": ("sbuf", [128, 84], "uint16"), "pfo": ("sbuf", [128, 56], "float32"),
+    "qo": ("sbuf", [128, 28], "float32"), "ku": ("sbuf", [128, 84], "uint16"),
     "nqk": ("sbuf", [128, 84], "float32"), "pkfk": ("sbuf", [128, 56], "float32"), "pku": ("sbuf", [128, 28], "uint16"),
     "xa": ("sbuf", [128, 28], "float32"), "w1": ("sbuf", [128, 28], "float32"), "w2": ("sbuf", [128, 28], "float32"),
     "xb": ("sbuf", [128, 28], "float32"), "xc": ("sbuf", [128, 28], "float32"),
@@ -168,18 +169,19 @@ def rank_program(g, core, T, topo):
     dma("y", T.vt[:, :], T.v[:, :], "l_v", [], [("vt", 0, 512)])
 
     op("g", lambda: g.iota(T.ip[:, :], [[0, 1]], 0, 1), [], [("ip", 0, 1)])
+    op("g", lambda: g.iota(T.i28[:, :], [[1, 28]], 0, 0, allow_small_or_imprecise_dtypes=True), [], [("i28", 0, 28)])
     op("g", lambda: g.iota(T.iot[:, :], [[1, C]], 0, 0, allow_small_or_imprecise_dtypes=True), [], [tab("iot")])
     op("g", lambda: g.iota(T.uoi[:, :], [[1, 2], [16, 8]], 0, 0), [], [("uoi", 0, 16)])
-    op("v", lambda: V.memset(T.ee[:, :], 0.0), [], [("ee", 0, 2048)])
-    op("v", lambda: V.memset(T.d0[:, :], 0.0), [], [("d0", 0, 224)] + [("d0o%d" % i, 0, 28) for i in range(4)])
-    op("v", lambda: V.memset(T.s30[:, :], 0.0), [], [("s30", 0, 84), ("s30f", 0, 28)])
+    op("v", lambda: V.memset(T.ee[:, 0:1024], 0.0), [], [("ee", 0, 1024)])
+    op("g", lambda: g.iota(T.d0[:, :], [[0, 224]], 0, 0, allow_small_or_imprecise_dtypes=True), [], [("d0", 0, 224)] + [("d0o%d" % i, 0, 28) for i in range(4)])
+    op("g", lambda: g.iota(T.s30[:, :], [[0, 84]], 0, 0, allow_small_or_imprecise_dtypes=True), [], [("s30", 0, 84), ("s30f", 0, 28)])
     cc = T.cc
     ts(T.ri[:, :], T.ip[:, :], 15, None, AluOpType.bitwise_and, None, [("ip", 0, 1)], [("ri", 0, 1)])
     cp(cc[:, 1:2], T.ip[:, :], [("ip", 0, 1)], [("cc", 1, 2)])
     cp(cc[:, 0:1], T.ri[:, :], [("ri", 0, 1)], [("cc", 0, 1)])
-    Rr, Rio = ("cc", 0, 1), tab("iot")
-    ts(T.dj[:, :], T.iot[:, 0:16], cc[:, 0:1], None, SUB, None, [Rr, Rio], [("dj", 0, 16)])
-    ts(T.roff[:, :], T.iot[:, 0:28], 0.0, cc[:, 0:1], MUL, ADD, [Rr, Rio], [("roff", 0, 28)])
+    Rr, Rio = ("cc", 0, 1), ("i28", 0, 28)
+    ts(T.dj[:, :], T.i28[:, 0:16], cc[:, 0:1], None, SUB, None, [Rr, Rio], [("dj", 0, 16)])
+    ts(T.roff[:, :], T.i28[:, 0:28], 0.0, cc[:, 0:1], MUL, ADD, [Rr, Rio], [("roff", 0, 28)])
     ts(cc[:, 4:5], cc[:, 0:1], 14.5, 1.0 - 1.0 / K, GE, MUL, [Rr], [("cc", 4, 5)])
     ts(cc[:, 5:6], cc[:, 0:1], 14.5, 0.5 - KF / 2, GE, MUL, [Rr], [("cc", 5, 6)])
     ts(T.c1[:, :], T.dj[:, :], 0.0, None, NE, None, [("dj", 0, 16)], [("c1", 0, 16)])
@@ -190,11 +192,13 @@ def rank_program(g, core, T, topo):
     ts(cc[:, 2:3], cc[:, 4:5], 1.0 / K, None, ADD, None, [("cc", 4, 5)], [("cc", 2, 3)])
     ts(cc[:, 3:4], cc[:, 5:6], KF / 2, None, ADD, None, [("cc", 5, 6)], [("cc", 3, 4)])
     SK, RSK, TH, RTH = cc[:, 2:3], ("cc", 2, 3), cc[:, 3:4], ("cc", 3, 4)
-    ts(T.qo[:, :], T.iot[:, 0:28], 16.0, cc[:, 0:1], MUL, ADD, [Rr, Rio], [("qo", 0, 28)])
+    ts(T.qo[:, :], T.i28[:, 0:28], 16.0, cc[:, 0:1], MUL, ADD, [Rr, Rio], [("qo", 0, 28)])
+    op("v", lambda: V.memset(T.ee[:, 1024:2048], 0.0), [], [("ee", 1024, 2048)])
     cp(T.uoff[:, :], T.uoi[:, :], [("uoi", 0, 16)], [("uoff", 0, 16)])
 
     cp(T.lu3[:, 28:56], T.ppi[:, :], [("ppi", 0, 28)], [("lu3", 28, 56)])
     cp(T.ku[:, :], T.pri[:, :], [("pri", 0, 84)], [("ku", 0, 84)])
+    op("s", lambda: S.activation(T.cf[:, :], T.c16[:, 0:16].indirect(T.roff[:, 0:28]), COPY), [("c16", 0, 16), ("roff", 0, 28)], [tab("cf")])
     look("s", "pw", "iot", "lu3", 28, 56)
     for b in range(4):
         ts(T.ee[:, 512 * b + b:512 * b + 512:4], T.iot[:, 0:128], cc[:, 1:2], None, EQ, None, [("cc", 1, 2), tab("iot"), ("ee", 0, 2048)], [("ee%d" % b, 0, 128)])
@@ -203,49 +207,57 @@ def rank_program(g, core, T, topo):
        [("qu", 0, 128), ("uoff", 0, 16)], [("qus", 0, 256)])
     op("s", lambda: S.activation(T.sus[:, 0:256], T.su[:, 0:128].indirect(T.uoff[:, 0:16]), COPY), [("su", 0, 128), ("uoff", 0, 16)], [("sus", 0, 256)])
     look("s", "pkw", "pw", "ku", 0, 28)
-    op("s", lambda: S.activation(T.cf[:, :], T.c16[:, 0:16].indirect(T.roff[:, 0:28]), COPY), [("c16", 0, 16), ("roff", 0, 28)], [tab("cf")])
+    op("s", lambda: S.activation(T.cb[:, :], T.c16[:, 16:32].indirect(T.roff[:, 0:28]), COPY), [("c16", 16, 32), ("roff", 0, 28)], [tab("cb")])
 
     def exchange(t):
         k = T.pri[:, 28 * t:28 * t + 28]
         tt(T["d1%d" % t][:, 0:56:2], k, T.qo[:, :], SUB, [("pri", 0, 84), ("qo", 0, 28)], [("d1d%d" % t, 0, 28)])
-        tt(T.nqk[:, 28 * t:28 * t + 28], T.qo[:, :], k, SUB, [("pri", 0, 84), ("qo", 0, 28)], [("nqk", 28 * t, 28 * t + 28)])
         cp(T["d1%d" % t][:, 1:56:2], T.qo[:, :], [("qo", 0, 28)], [("d1b%d" % t, 0, 28)])
 
-    def prep_p(t, lu):
-        d1 = T["d1%d" % t]
+    def displace(t):
+        k = T.pri[:, 28 * t:28 * t + 28]
+        tt(T.nqk[:, 28 * t:28 * t + 28], T.qo[:, :], k, SUB, [("pri", 0, 84), ("qo", 0, 28)], [("nqk", 28 * t, 28 * t + 28)])
+
+    def copy(q, d, s, R, W):
+        if q == "g":
+            op("g", lambda: g.affine_select(d, s, [[0, 28]], GT, 0.0, 1, 0), R, W)
+        else:
+            cp(d, s, R, W)
+
+    def base(q, t, i, X):
+        copy(q, T["d1%d" % t][:, 56 * i + 1:56 * i + 56:2], X[0], [X[1]], [("d1b%d" % t, 28 * i, 28 * i + 28)])
+
+    def prep_p(t, P):
         ts(T.pku[:, :], T.pks[:, 15:C:16], SK, None, MUL, None, [("pks", 0, C), RSK], [("pku", 0, 28)])
         ts(T.pkfk[:, 0:28], T.pks[:, 15:C:16], SK, None, MUL, None, [("pks", 0, C), RSK], [("pkfk", 0, 28)])
-        cp(T.pfo[:, 0:28], T[lu][:, 28:56], [(lu, 28, 56)], [("pfo", 0, 28)])
-        exchange(t)
-        tt(d1[:, 56:112:2], T.pkfk[:, 0:28], T.pfo[:, 0:28], SUB, [("pkfk", 0, 28), ("pfo", 0, 28)], [("d1d%d" % t, 28, 56)])
-        cp(d1[:, 57:112:2], T.pfo[:, 0:28], [("pfo", 0, 28)], [("d1b%d" % t, 28, 56)])
+        yield
+        tt(T["d1%d" % t][:, 56:112:2], T.pkfk[:, 0:28], P[0], SUB, [("pkfk", 0, 28), P[1]], [("d1d%d" % t, 28, 56)])
+        yield
 
-    def prep_f(t, lu):
+    def prep_f(t, F):
         d1 = T["d1%d" % t]
-        cp(T.pfo[:, 28:56], T[lu][:, 56:84], [(lu, 56, 84)], [("pfo", 28, 56)])
         ts(T.pkfk[:, 28:56], T.pks[:, C + 15:2 * C:16], SK, None, MUL, None, [("pks", C, 2 * C), RSK], [("pkfk", 28, 56)])
         yield
-        cp(d1[:, 113:168:2], T.pfo[:, 28:56], [("pfo", 28, 56)], [("d1b%d" % t, 56, 84)])
         tt(T.xa[:, :], T.pkfk[:, 28:56], T.nqk[:, 28 * t:28 * t + 28], ADD, [("pkfk", 28, 56), ("nqk", 28 * t, 28 * t + 28)], [("xa", 0, 28)])
-        tt(d1[:, 112:168:2], T.pkfk[:, 28:56], T.pfo[:, 28:56], SUB, [("pkfk", 28, 56), ("pfo", 28, 56)], [("d1d%d" % t, 56, 84)])
+        tt(d1[:, 112:168:2], T.pkfk[:, 28:56], F[0], SUB, [("pkfk", 28, 56), F[1]], [("d1d%d" % t, 56, 84)])
         yield
         ts(T.w1[:, :], T.xa[:, :], -0.5, 448.0, LT, MUL, [("xa", 0, 28)], [("w1", 0, 28)])
         ts(T.w2[:, :], T.xa[:, :], 447.5, -448.0, GE, MUL, [("xa", 0, 28)], [("w2", 0, 28)])
         yield
-        tt(T.xb[:, :], T.xa[:, :], T.pfo[:, 28:56], SUB, [("xa", 0, 28), ("pfo", 28, 56)], [("xb", 0, 28)])
+        tt(T.xb[:, :], T.xa[:, :], F[0], SUB, [("xa", 0, 28), F[1]], [("xb", 0, 28)])
         tt(T.xc[:, :], T.w1[:, :], T.w2[:, :], ADD, [("w1", 0, 28), ("w2", 0, 28)], [("xc", 0, 28)])
-        cp(d1[:, 169:224:2], T.pfo[:, 28:56], [("pfo", 28, 56)], [("d1b%d" % t, 84, 112)])
         yield
         tt(d1[:, 168:224:2], T.xb[:, :], T.xc[:, :], ADD, [("xb", 0, 28), ("xc", 0, 28)], [("d1d%d" % t, 84, 112)])
         yield
 
+    P0, F0 = (T.ppi[:, :], ("ppi", 0, 28)), (T.rfi[:, :], ("rfi", 0, 28))
+    P1, F1 = (T.do[:, 57:112:2], ("do", 0, 112)), (T.s3o[:, 2:84:3], ("s3o", 0, 84))
     op("v", lambda: V.quantize_mx(T.qx[:, 0:H], T.sx[:, 0:H], T.xin[:, 0:4 * H]), [("xin", 0, 4 * H)], [("qx", 0, H), ("sx", 0, H)])
     op("v", lambda: V.quantize_mx(T.qx[:, H:C], T.sx[:, H:C], T.xin[:, 4 * H:4 * C]), [("xin", 4 * H, 4 * C)], [("qx", H, C), ("sx", H, C)])
-    op("v", lambda: V.quantize_mx(T.qe[:, :], T.se[:, :], T.ee[:, :]), [("ee", 0, 2048)] + [("ee%d" % b, 0, 128) for b in range(4)], [("qe", 0, 512), ("se", 0, 512)])
     scan("pkw", "pks", 0)
-    prep_p(0, "lu3")
-    cp(T.lu3[:, 56:84], T.rfi[:, :], [("rfi", 0, 28)], [("lu3", 56, 84)])
-    ts(T.s30[:, 1:84:3], T.iot[:, 0:28], 0.0, SK, MUL, ADD, [RSK, Rio, ], [("s30", 0, 84)])
+    pre = prep_p(0, P0)
+    next(pre)
+    op("v", lambda: V.quantize_mx(T.qe[:, :], T.se[:, :], T.ee[:, :]), [("ee", 0, 2048)] + [("ee%d" % b, 0, 128) for b in range(4)], [("qe", 0, 512), ("se", 0, 512)])
 
     def mm(bank, n, st, sts, a, mv, mvs, lo):
         op("t", lambda: g.tensor.matmul_mx(T["ps%d" % bank][:, 0:n], T[st][:, a:a + 128], T[sts][:, a:a + 128], T[mv][:, lo:lo + n], T[mvs][:, lo:lo + n], True, True),
@@ -292,27 +304,33 @@ def rank_program(g, core, T, topo):
         d1 = T["d1%d" % t]
         for h in range(2):
             mm(2 + h, H, "qus", "sus", 0, "qx", "sx", H * h)
-        for b in range(4):
-            mm(FB[b], C, "qe", "se", 128 * b, "qx", "sx", 0)
-        mm(6, C, "qus", "sus", 128, "qx", "sx", 0)
         for h in range(2):
             op("s", lambda: S.activation(T.sa[:, H * h:H * h + H], T["ps%d" % (2 + h)][:, 0:H], SIGN), [("ps%d" % (2 + h), 0, 512)], [("sa", H * h, H * h + H)])
-        if t == 0:
-            op("s", lambda: S.activation(T.cb[:, :], T.c16[:, 16:32].indirect(T.roff[:, 0:28]), COPY), [("c16", 16, 32), ("roff", 0, 28)], [tab("cb")])
         look("s", "h2", "sa", "pku")
         if t == 0:
+            cp(T.lu3[:, 56:84], T.rfi[:, :], [("rfi", 0, 28)], [("lu3", 56, 84)])
             look("s", "fw", "iot", "lu3", 56, 84)
             look("s", "fkw", "fw", "ku", 0, 28)
         else:
             scan("fkw", "pks", C)
-        rest = prep_f(t, lp)
+        rest = prep_f(t, F1 if t else F0)
+        if t > 0:
+            next(rest)
+            next(rest)
         look("v", "h1", "sa", lp, 28, 56)
-        if t > 0:
-            next(rest)
+        if t == 0:
+            next(pre)
+            base("v", 0, 2, F0)
         scan("h1", "hs", 0, True)
+        if t == 0:
+            base("v", 0, 3, F0)
+            base("v", 0, 1, P0)
+            exchange(0)
+            displace(0)
         scan("h2", "hs", C, True)
-        if t > 0:
-            next(rest)
+        for b in range(4):
+            mm(FB[b], C, "qe", "se", 128 * b, "qx", "sx", 0)
+        mm(6, C, "qus", "sus", 128, "qx", "sx", 0)
         for b in range(3):
             evac("s", FB[b], C, "fp", C * b, ("fp", C * b, C * b + C), None)
         op("s", lambda: S.activation(T.bs[:, :], T.ps6[:, 0:C], SIGN), [("ps6", 0, 512)], [tab("bs")])
@@ -330,6 +348,8 @@ def rank_program(g, core, T, topo):
         if t > 0:
             next(rest)
         cp(T[lu][:, 0:56], T.do[:, 1:112:2], [("do", 0, 112)], [(lu, 0, 56)])
+        if not last:
+            base("g", t + 1, 1, P1)
         if t == 0:
             scan("fkw", "pks", C)
         for _i in rest:
@@ -341,7 +361,9 @@ def rank_program(g, core, T, topo):
         look("s", "tcw", "tw", "cu")
         look("s", "hb", "bs", lu, 28, 56)
         gather_g("v", 0, lu)
-        cp(T.s31[:, 2:84:3], T.do[:, 169:224:2], [("do", 112, 224)], [("s31c", 0, 28)])
+        copy("g", T.s31[:, 2:84:3], T.do[:, 169:224:2], [("do", 112, 224)], [("s31c", 0, 28)])
+        if t == 0:
+            ts(T.s30[:, 1:84:3], T.i28[:, 0:28], 0.0, SK, MUL, ADD, [RSK, Rio], [("s30", 0, 84)])
         ts(T.s31[:, 1:84:3], T.do[:, 169:224:2], -1.0, None, MUL, None, [("do", 112, 224)], [("s31b", 0, 28)])
         gather_g("v", 1, lu)
         addend(0)
@@ -362,6 +384,9 @@ def rank_program(g, core, T, topo):
         landed("fr%d" % t, len(fe), [("fs%d" % t, 0, 28)])
         qz, sz, qy, sy = "qzu%d" % t, "szu%d" % t, "qy%d" % t, "sy%d" % t
         addend(2)
+        if not last:
+            base("g", t + 1, 2, F1)
+            base("g", t + 1, 3, F1)
         for h in (1, 0):
             for b in range(4):
                 src = T.gp[:, C * b:C * b + C].indirect(T[lu][:, 56 + 14 * h:70 + 14 * h])
@@ -370,6 +395,11 @@ def rank_program(g, core, T, topo):
                 if h and b == 1:
                     addend(3)
             R = [("zt%d" % b, H * h, H * h + H) for b in range(4)]
+            if not last:
+                if h:
+                    exchange(t + 1)
+                else:
+                    displace(t + 1)
             if h:
                 op("v", lambda: V.quantize_mx(T[qz][:, :], T[sz][:, :], T.zt[:, 4 * H:4 * C]), R, [(qz, 0, H), (sz, 0, H)])
                 need("g", [(qz, 0, H), (sz, 0, H)], [])
@@ -398,51 +428,54 @@ def rank_program(g, core, T, topo):
         look("s", "c2w", "fsw", lu, 56, 84)
         for b in range(4):
             mm(2 + b % 2, H, "qw", "sw", 128 * b, qy, sy, 0)
-            if b == 2:
+            if b == (0 if t == 1 else 2):
                 look("s", "ew", "c2w", in_)
-            evac("v" if last or (t == 0 and b % 2 == 1) else "s", 2 + b % 2, H, "bp", C * b, ("bp", C * b, C * b + H), 0.03125)
+            evac("v" if (last and b > 1) or (t == 1 and b < 2) else "s", 2 + b % 2, H, "bp", C * b, ("bp", C * b, C * b + H), 0.03125)
         if not last:
             scan("pkw", "pks", 0)
-            prep_p(t + 1, lu)
+            for _i in prep_p(t + 1, P1):
+                pass
         else:
-            look("s", "fw", "iot", lu, 56, 84)
             dma("y", T.pf[:, 0:C], T.pw[0:128:16, :], "outy", [tab("pw")], [])
-            dma("y", T.pf[:, C:2 * C], T.fw[0:128:16, :], "outy", [tab("fw")], [])
             op("v", lambda: V.quantize_mx(T.qv[:, :], T.sv[:, :], T.vt[:, :]), [("vt", 0, 512)], [("qv", 0, 128), ("sv", 0, 128)])
         scan("ew", "es")
         ts(T.eu[:, :], T.es[:, 15:C:16], SK, None, MUL, None, [tab("es"), RSK], [("eu", 0, 28)])
         for b in range(4):
             mm(4 + b, H, "qw", "sw", 128 * b, qy, sy, H)
-            evac("v" if b % 2 == 0 else "s", 4 + b, H, "bp", C * b + H, ("bp", C * b + H, C * b + C), 0.03125)
-        for lo, hi in ([(0, H), (H, C)] if last else [(0, C)]):
+            evac("s", 4 + b, H, "bp", C * b + H, ("bp", C * b + H, C * b + C), 0.03125)
+        VP = 2 if last else 3
+        for lo, hi in ([(0, CUT), (CUT, C)] if last else [(0, C)]):
             a, e = lo // 16, hi // 16
-            for b in (2, 3):
+            for b in range(VP, 4):
                 op("s", lambda: S.activation(T.tmp[:, C * (b - 2) + lo:C * (b - 2) + hi], T.bp[:, C * b:C * b + C].indirect(T.eu[:, a:e]), COPY),
                    [("bp", C * b, C * b + C), ("eu", 0, 28)], [("tmp", C * (b - 2) + lo, C * (b - 2) + hi)])
-            if not last:
+            if lo == 0:
                 look("s", "fw", "iot", lu, 56, 84)
+            if last and lo == 0:
+                dma("y", T.pf[:, C:2 * C], T.fw[0:128:16, :], "outy", [tab("fw")], [])
+            if not last:
                 look("s", "fkw", "fw", "ku", 28 * t + 28, 28 * t + 56)
             for b in range(4):
                 dst_ = T.xt[:, 4 * lo + b:4 * hi:4]
-                if b < 2:
+                if b < VP:
                     tt(dst_, T.bp[:, C * b:C * b + C].indirect(T.eu[:, a:e]), T.fp[:, C * b + lo:C * b + hi], ADD,
                        [("bp", C * b, C * b + C), ("eu", 0, 28), ("fp", C * b, C * b + C)], [("xt%d" % b, lo, hi)])
                 else:
                     tt(dst_, T.tmp[:, C * (b - 2) + lo:C * (b - 2) + hi], T["ps%d" % FB[b]][:, lo:hi], ADD,
                        [("tmp", C * (b - 2) + lo, C * (b - 2) + hi), ("ps%d" % FB[b], 0, 512)], [("xt%d" % b, lo, hi)])
-            for i in range(lo, hi, H):
-                op("v", lambda: V.quantize_mx(T.qx[:, i:i + H], T.sx[:, i:i + H], T.xt[:, 4 * i:4 * i + 4 * H]),
-                   [("xt%d" % b, lo, hi) for b in range(4)], [("qx", i, i + H), ("sx", i, i + H)])
+            for i, j in ([(lo, hi)] if last else [(0, H), (H, C)]):
+                op("v", lambda: V.quantize_mx(T.qx[:, i:j], T.sx[:, i:j], T.xt[:, 4 * i:4 * j]),
+                   [("xt%d" % b, lo, hi) for b in range(4)], [("qx", i, j), ("sx", i, j)])
             if last:
-                mm(6 + lo // H, H, "qv", "sv", 0, "qx", "sx", lo)
+                mm(7 if lo else 6, hi - lo, "qv", "sv", 0, "qx", "sx", lo)
                 dma("y", T.oc[:, 4 * lo:4 * hi], T.qx[:, lo:hi].bitcast(dt.uint8), "outy", [("qx", lo, hi)], [])
                 if hi == C:
                     for i in range(4):
                         dma("y", T.osc[4 * i:4 * i + 4, :], T.sx[32 * i:32 * i + 4, :], "outy", [("sx", 0, C)], [])
         if last:
-            for h in range(2):
-                evac("s", 6 + h, H, "ysb", H * h, ("ysb", H * h, H * h + H), None)
-                dma("s", T.y[:, H * h:H * h + H], T.ysb[:, H * h:H * h + H], "outs", [("ysb", H * h, H * h + H)], [])
+            for i, j, n in ((0, CUT, 6), (CUT, C, 7)):
+                evac("s", n, j - i, "ysb", i, ("ysb", i, j), None)
+                dma("s", T.y[:, i:j], T.ysb[:, i:j], "outs", [("ysb", i, j)], [])
     for sem in sorted(total):
         if waited.get(sem, 0) < total[sem]:
             g.wait_ge(T.sem[sem], total[sem])

from concourse.bass import DstId, RemoteDMATransfer
from concourse.mybir import dt, AluOpType, ActivationFunctionType

C, H = 448, 224
CUT = 320
STEP = [1, 2, 3]
ADD, SUB, MUL = AluOpType.add, AluOpType.subtract, AluOpType.mult
GT, GE, LT, EQ, NE = AluOpType.is_gt, AluOpType.is_ge, AluOpType.is_lt, AluOpType.is_equal, AluOpType.not_equal
COPY, SIGN = ActivationFunctionType.Copy, ActivationFunctionType.Sign
K = 16384.0
KF = 32.0
CODES = "float8_e4m3fn_x4"

SCRATCH = {
    "xin": ("sbuf", [128, 4 * C], "bfloat16"), "xt": ("sbuf", [128, 4 * C], "bfloat16"), "zt": ("sbuf", [128, 4 * C], "bfloat16"),
    "ut": ("sbuf", [128, 512], "bfloat16"), "vt": ("sbuf", [128, 512], "bfloat16"), "ee": ("sbuf", [128, 2048], "bfloat16"),
    "qx": ("sbuf", [128, C], CODES), "sx": ("sbuf", [128, C], "uint8"),
    "qu": ("sbuf", [128, 128], CODES), "su": ("sbuf", [128, 128], "uint8"),
    "qus": ("sbuf", [128, 256], CODES), "sus": ("sbuf", [128, 256], "uint8"),
    "qv": ("sbuf", [128, 128], CODES), "sv": ("sbuf", [128, 128], "uint8"),
    "qe": ("sbuf", [128, 512], CODES), "se": ("sbuf", [128, 512], "uint8"),
    "qw": ("sbuf", [128, 512], CODES), "sw": ("sbuf", [128, 512], "uint8"),
    "fp": ("sbuf", [128, 4 * C], "bfloat16"), "gp": ("sbuf", [128, 4 * C], "bfloat16"), "bp": ("sbuf", [128, 4 * C], "bfloat16"),
    "g2": ("sbuf", [128, 4 * C], "bfloat16"), "tmp": ("sbuf", [128, 2 * C], "bfloat16"), "ysb": ("sbuf", [128, C], "float32"),
    "ip": ("sbuf", [128, 1], "int32"), "ri": ("sbuf", [128, 1], "int32"), "cc": ("sbuf", [128, 8], "float32"),
    "i28": ("sbuf", [128, 28], "float32"), "iot": ("sbuf", [128, C], "float32"), "dj": ("sbuf", [128, 16], "float32"),
    "c1": ("sbuf", [128, 16], "float32"), "c2": ("sbuf", [128, 32], "float32"), "c16": ("sbuf", [128, 32], "float32"),
    "roff": ("sbuf", [128, 28], "uint16"), "cf": ("sbuf", [128, C], "float32"), "cb": ("sbuf", [128, C], "bfloat16"),
    "uoi": ("sbuf", [128, 16], "int32"), "uoff": ("sbuf", [128, 16], "uint16"),
    "ppi": ("sbuf", [128, 28], "int32"), "rfi": ("sbuf", [128, 28], "int32"), "pri": ("sbuf", [128, 84], "int32"),
    "qo": ("sbuf", [128, 28], "float32"), "ku": ("sbuf", [128, 84], "uint16"),
    "nqk": ("sbuf", [128, 84], "float32"), "pkfk": ("sbuf", [128, 56], "float32"), "pku": ("sbuf", [128, 28], "uint16"),
    "xa": ("sbuf", [128, 28], "float32"), "w1": ("sbuf", [128, 28], "float32"), "w2": ("sbuf", [128, 28], "float32"),
    "xb": ("sbuf", [128, 28], "float32"), "xc": ("sbuf", [128, 28], "float32"),
    "d0": ("sbuf", [128, 224], "float32"), "do": ("sbuf", [128, 224], "float32"),
    "s30": ("sbuf", [128, 84], "float32"), "s31": ("sbuf", [128, 84], "float32"), "s3o": ("sbuf", [128, 84], "float32"),
    "sa": ("sbuf", [128, C], "bfloat16"), "bs": ("sbuf", [128, C], "bfloat16"),
    "h1": ("sbuf", [128, C], "bfloat16"), "h2": ("sbuf", [128, C], "bfloat16"), "hb": ("sbuf", [128, C], "bfloat16"),
    "hs": ("sbuf", [128, 2 * C], "bfloat16"), "hbs": ("sbuf", [128, C], "bfloat16"), "fl": ("sbuf", [128, 56], "float32"),
    "cu": ("sbuf", [128, 28], "uint16"), "eu": ("sbuf", [128, 28], "uint16"),
    "tw": ("sbuf", [128, C], "float32"), "tcw": ("sbuf", [128, C], "float32"), "tcs": ("sbuf", [128, C], "float32"),
    "inw": ("sbuf", [128, C], "float32"), "ins": ("sbuf", [128, C], "float32"),
    "pw": ("sbuf", [128, C], "float32"), "fw": ("sbuf", [128, C], "float32"),
    "pkw": ("sbuf", [128, C], "float32"), "fkw": ("sbuf", [128, C], "float32"), "pks": ("sbuf", [128, 2 * C], "float32"),
    "fsw": ("sbuf", [128, C], "float32"), "c2w": ("sbuf", [128, C], "float32"),
    "ew": ("sbuf", [128, C], "float32"), "es": ("sbuf", [128, C], "float32"),
}
for _t in range(3):
    SCRATCH["d1%d" % _t] = ("sbuf", [128, 224], "float32")
    SCRATCH["qzu%d" % _t] = ("sbuf", [128, H], CODES)
    SCRATCH["szu%d" % _t] = ("sbuf", [128, H], "uint8")
    SCRATCH["qy%d" % _t] = ("sbuf", [128, C], CODES)
    SCRATCH["sy%d" % _t] = ("sbuf", [128, C], "uint8")
    SCRATCH["fs%d" % _t] = ("sbuf", [128, 28], "uint16")
    SCRATCH["inv%d" % _t] = ("sbuf", [128, 28], "uint16")
for _t in range(4):
    SCRATCH["lu%d" % _t] = ("sbuf", [128, 84], "uint16")
for _t in range(8):
    SCRATCH["ps%d" % _t] = ("psum", [128, 512], "float32")

LOADS = ["pp", "rf", "pr", "u", "v", "x0", "x1", "wc", "ws", "g0", "g1", "g2", "g3"]
SEMAPHORES = ["kv", "ks", "kt", "kg", "loc", "outy", "outs"] + ["l_" + n for n in LOADS] + \
    ["fr%d" % t for t in range(3)] + ["zr%d" % t for t in range(3)]


def rank_program(g, core, T, topo):
    rank = T.rank_of(core)
    if rank is None:
        return
    Q = {"v": g.vector, "s": g.scalar, "t": g.tensor, "g": g, "y": g.sync}
    OWN = {"v": "kv", "s": "ks", "t": "kt", "g": "kg"}
    known = {q: {} for q in Q}
    total = {}
    waited = {}
    recs = {}

    def wait(q, sem, val, clk):
        Q[q].wait_ge(T.sem[sem], val)
        waited[sem] = max(waited.get(sem, 0), val)
        for k in clk:
            known[q][k] = max(known[q].get(k, 0), clk[k])

    def need(q, R, W):
        req = {}
        for w, regs in ((False, R), (True, W)):
            for b, lo, hi in regs:
                excl = w or b[:2] == "ps"
                for r in recs.get(b, []):
                    if r[0] < hi and lo < r[1] and (r[5] or excl) and not (r[4] == q and not r[5]):
                        sem, val = r[2]
                        if known[q].get(sem, 0) < val and (sem not in req or req[sem][0] < val):
                            req[sem] = (val, r[3])
        for sem in sorted(req):
            val, clk = req[sem]
            if known[q].get(sem, 0) >= val:
                continue
            if any(o != sem and known[q].get(o, 0) < req[o][0] and req[o][1].get(sem, 0) >= val for o in req):
                continue
            wait(q, sem, val, clk)

    def note(q, R, W, tok, clk):
        for w, regs in ((False, R), (True, W)):
            for b, lo, hi in regs:
                l = recs.setdefault(b, [])
                if w:
                    l = [r for r in l if not (lo <= r[0] and r[1] <= hi)]
                else:
                    l = [r for r in l if not (r[4] == q and not r[5] and lo <= r[0] and r[1] <= hi)]
                l.append((lo, hi, tok, clk, q, w))
                recs[b] = l

    def op(q, make, R, W):
        need(q, R, W)
        sem = OWN[q]
        total[sem] = total.get(sem, 0) + 1
        make().then_inc(T.sem[sem], 1)
        clk = dict(known[q])
        clk[sem] = total[sem]
        note(q, R, W, (sem, total[sem]), clk)

    def dma(q, out, in_, sem, R, W):
        need(q, R, W)
        total[sem] = total.get(sem, 0) + 16
        Q[q].dma_start(out, in_).then_inc(T.sem[sem], 16)
        clk = dict(known[q])
        clk[sem] = total[sem]
        note("d" + q, R, W, (sem, total[sem]), clk)

    def landed(sem, val, W):
        total[sem] = val
        note("remote", [], W, (sem, val), {sem: val})

    V, S = g.vector, g.scalar

    def tab(n):
        return (n, 0, C)

    def look(q, out, win, off, a=0, b=28):
        src = T[win][:, 0:C].indirect(T[off][:, a:b])

        def make():
            return S.activation(T[out][:, :], src, COPY) if q == "s" else V.tensor_copy(T[out][:, :], src)
        op(q, make, [tab(win), (off, a, b)], [tab(out)])

    def scan(src, out, o=0, flags=False):
        c = "cb" if flags else "cf"
        op("v", lambda: V.tensor_tensor_scan(T[out][:, o:o + C], T[c][:, :], T[src][:, :], 0.0, MUL, ADD), [tab(src), tab(c)], [(out, o, o + C)])

    def ts(out, in0, s1, s2, o0, o1, R, W):
        if o1 is None:
            op("v", lambda: V.tensor_scalar(out, in0, s1, None, o0), R, W)
        else:
            op("v", lambda: V.tensor_scalar(out, in0, s1, s2, o0, o1), R, W)

    def tt(out, a, b, o, R, W):
        op("v", lambda: V.tensor_tensor(out, a, b, o), R, W)

    def cp(out, a, R, W):
        op("v", lambda: V.tensor_copy(out, a), R, W)

    dma("y", T.ppi[:, :], T.pp[:, :], "l_pp", [], [("ppi", 0, 28)])
    dma("s", T.pri[:, :], T.pr[:, :], "l_pr", [], [("pri", 0, 84)])
    dma("y", T.xin[:, 0:4 * H], T.x[:, 0:4 * H], "l_x0", [], [("xin", 0, 4 * H)])
    dma("s", T.ut[:, :], T.u[:, :], "l_u", [], [("ut", 0, 512)])
    dma("y", T.xin[:, 4 * H:4 * C], T.x[:, 4 * H:4 * C], "l_x1", [], [("xin", 4 * H, 4 * C)])
    dma("y", T.rfi[:, :], T.rf[:, :], "l_rf", [], [("rfi", 0, 28)])
    dma("y", T.qw[:, :].bitcast(dt.uint8), T.wc[:, :], "l_wc", [], [("qw", 0, 512)])
    dma("y", T.sw[:, :], T.ws[:, :], "l_ws", [], [("sw", 0, 512)])
    dma("y", T.vt[:, :], T.v[:, :], "l_v", [], [("vt", 0, 512)])

    op("g", lambda: g.iota(T.ip[:, :], [[0, 1]], 0, 1), [], [("ip", 0, 1)])
    op("g", lambda: g.iota(T.i28[:, :], [[1, 28]], 0, 0, allow_small_or_imprecise_dtypes=True), [], [("i28", 0, 28)])
    op("g", lambda: g.iota(T.iot[:, :], [[1, C]], 0, 0, allow_small_or_imprecise_dtypes=True), [], [tab("iot")])
    op("g", lambda: g.iota(T.uoi[:, :], [[1, 2], [16, 8]], 0, 0), [], [("uoi", 0, 16)])
    op("v", lambda: V.memset(T.ee[:, 0:1024], 0.0), [], [("ee", 0, 1024)])
    op("g", lambda: g.iota(T.d0[:, :], [[0, 224]], 0, 0, allow_small_or_imprecise_dtypes=True), [], [("d0", 0, 224)] + [("d0o%d" % i, 0, 28) for i in range(4)])
    op("g", lambda: g.iota(T.s30[:, :], [[0, 84]], 0, 0, allow_small_or_imprecise_dtypes=True), [], [("s30", 0, 84), ("s30f", 0, 28)])
    cc = T.cc
    ts(T.ri[:, :], T.ip[:, :], 15, None, AluOpType.bitwise_and, None, [("ip", 0, 1)], [("ri", 0, 1)])
    cp(cc[:, 1:2], T.ip[:, :], [("ip", 0, 1)], [("cc", 1, 2)])
    cp(cc[:, 0:1], T.ri[:, :], [("ri", 0, 1)], [("cc", 0, 1)])
    Rr, Rio = ("cc", 0, 1), ("i28", 0, 28)
    ts(T.dj[:, :], T.i28[:, 0:16], cc[:, 0:1], None, SUB, None, [Rr, Rio], [("dj", 0, 16)])
    ts(T.roff[:, :], T.i28[:, 0:28], 0.0, cc[:, 0:1], MUL, ADD, [Rr, Rio], [("roff", 0, 28)])
    ts(cc[:, 4:5], cc[:, 0:1], 14.5, 1.0 - 1.0 / K, GE, MUL, [Rr], [("cc", 4, 5)])
    ts(cc[:, 5:6], cc[:, 0:1], 14.5, 0.5 - KF / 2, GE, MUL, [Rr], [("cc", 5, 6)])
    ts(T.c1[:, :], T.dj[:, :], 0.0, None, NE, None, [("dj", 0, 16)], [("c1", 0, 16)])
    ts(T.c2[:, 0:16], T.dj[:, :], 1.0, K - 1.0, EQ, MUL, [("dj", 0, 16)], [("c2", 0, 16)])
    ts(T.c2[:, 16:32], T.dj[:, :], 1.0, KF - 1.0, EQ, MUL, [("dj", 0, 16)], [("c2", 16, 32)])
    tt(T.c16[:, 0:16], T.c1[:, :], T.c2[:, 0:16], ADD, [("c1", 0, 16), ("c2", 0, 16)], [("c16", 0, 16)])
    tt(T.c16[:, 16:32], T.c1[:, :], T.c2[:, 16:32], ADD, [("c1", 0, 16), ("c2", 16, 32)], [("c16", 16, 32)])
    ts(cc[:, 2:3], cc[:, 4:5], 1.0 / K, None, ADD, None, [("cc", 4, 5)], [("cc", 2, 3)])
    ts(cc[:, 3:4], cc[:, 5:6], KF / 2, None, ADD, None, [("cc", 5, 6)], [("cc", 3, 4)])
    SK, RSK, TH, RTH = cc[:, 2:3], ("cc", 2, 3), cc[:, 3:4], ("cc", 3, 4)
    ts(T.qo[:, :], T.i28[:, 0:28], 16.0, cc[:, 0:1], MUL, ADD, [Rr, Rio], [("qo", 0, 28)])
    op("v", lambda: V.memset(T.ee[:, 1024:2048], 0.0), [], [("ee", 1024, 2048)])
    cp(T.uoff[:, :], T.uoi[:, :], [("uoi", 0, 16)], [("uoff", 0, 16)])

    cp(T.lu3[:, 28:56], T.ppi[:, :], [("ppi", 0, 28)], [("lu3", 28, 56)])
    cp(T.ku[:, :], T.pri[:, :], [("pri", 0, 84)], [("ku", 0, 84)])
    op("s", lambda: S.activation(T.cf[:, :], T.c16[:, 0:16].indirect(T.roff[:, 0:28]), COPY), [("c16", 0, 16), ("roff", 0, 28)], [tab("cf")])
    look("s", "pw", "iot", "lu3", 28, 56)
    for b in range(4):
        ts(T.ee[:, 512 * b + b:512 * b + 512:4], T.iot[:, 0:128], cc[:, 1:2], None, EQ, None, [("cc", 1, 2), tab("iot"), ("ee", 0, 2048)], [("ee%d" % b, 0, 128)])
    op("v", lambda: V.quantize_mx(T.qu[:, :], T.su[:, :], T.ut[:, :]), [("ut", 0, 512)], [("qu", 0, 128), ("su", 0, 128)])
    op("v", lambda: V.tensor_copy(T.qus[:, 0:256].bitcast(dt.uint32), T.qu[:, 0:128].bitcast(dt.uint32).indirect(T.uoff[:, 0:16])),
       [("qu", 0, 128), ("uoff", 0, 16)], [("qus", 0, 256)])
    op("s", lambda: S.activation(T.sus[:, 0:256], T.su[:, 0:128].indirect(T.uoff[:, 0:16]), COPY), [("su", 0, 128), ("uoff", 0, 16)], [("sus", 0, 256)])
    look("s", "pkw", "pw", "ku", 0, 28)
    op("s", lambda: S.activation(T.cb[:, :], T.c16[:, 16:32].indirect(T.roff[:, 0:28]), COPY), [("c16", 16, 32), ("roff", 0, 28)], [tab("cb")])

    def exchange(t):
        k = T.pri[:, 28 * t:28 * t + 28]
        tt(T["d1%d" % t][:, 0:56:2], k, T.qo[:, :], SUB, [("pri", 0, 84), ("qo", 0, 28)], [("d1d%d" % t, 0, 28)])
        cp(T["d1%d" % t][:, 1:56:2], T.qo[:, :], [("qo", 0, 28)], [("d1b%d" % t, 0, 28)])

    def displace(t):
        k = T.pri[:, 28 * t:28 * t + 28]
        tt(T.nqk[:, 28 * t:28 * t + 28], T.qo[:, :], k, SUB, [("pri", 0, 84), ("qo", 0, 28)], [("nqk", 28 * t, 28 * t + 28)])

    def copy(q, d, s, R, W):
        if q == "g":
            op("g", lambda: g.affine_select(d, s, [[0, 28]], GT, 0.0, 1, 0), R, W)
        else:
            cp(d, s, R, W)

    def base(q, t, i, X):
        copy(q, T["d1%d" % t][:, 56 * i + 1:56 * i + 56:2], X[0], [X[1]], [("d1b%d" % t, 28 * i, 28 * i + 28)])

    def prep_p(t, P):
        ts(T.pku[:, :], T.pks[:, 15:C:16], SK, None, MUL, None, [("pks", 0, C), RSK], [("pku", 0, 28)])
        ts(T.pkfk[:, 0:28], T.pks[:, 15:C:16], SK, None, MUL, None, [("pks", 0, C), RSK], [("pkfk", 0, 28)])
        yield
        tt(T["d1%d" % t][:, 56:112:2], T.pkfk[:, 0:28], P[0], SUB, [("pkfk", 0, 28), P[1]], [("d1d%d" % t, 28, 56)])
        yield

    def prep_f(t, F):
        d1 = T["d1%d" % t]
        ts(T.pkfk[:, 28:56], T.pks[:, C + 15:2 * C:16], SK, None, MUL, None, [("pks", C, 2 * C), RSK], [("pkfk", 28, 56)])
        yield
        tt(T.xa[:, :], T.pkfk[:, 28:56], T.nqk[:, 28 * t:28 * t + 28], ADD, [("pkfk", 28, 56), ("nqk", 28 * t, 28 * t + 28)], [("xa", 0, 28)])
        tt(d1[:, 112:168:2], T.pkfk[:, 28:56], F[0], SUB, [("pkfk", 28, 56), F[1]], [("d1d%d" % t, 56, 84)])
        yield
        ts(T.w1[:, :], T.xa[:, :], -0.5, 448.0, LT, MUL, [("xa", 0, 28)], [("w1", 0, 28)])
        ts(T.w2[:, :], T.xa[:, :], 447.5, -448.0, GE, MUL, [("xa", 0, 28)], [("w2", 0, 28)])
        yield
        tt(T.xb[:, :], T.xa[:, :], F[0], SUB, [("xa", 0, 28), F[1]], [("xb", 0, 28)])
        tt(T.xc[:, :], T.w1[:, :], T.w2[:, :], ADD, [("w1", 0, 28), ("w2", 0, 28)], [("xc", 0, 28)])
        yield
        tt(d1[:, 168:224:2], T.xb[:, :], T.xc[:, :], ADD, [("xb", 0, 28), ("xc", 0, 28)], [("d1d%d" % t, 84, 112)])
        yield

    P0, F0 = (T.ppi[:, :], ("ppi", 0, 28)), (T.rfi[:, :], ("rfi", 0, 28))
    P1, F1 = (T.do[:, 57:112:2], ("do", 0, 112)), (T.s3o[:, 2:84:3], ("s3o", 0, 84))
    op("v", lambda: V.quantize_mx(T.qx[:, 0:H], T.sx[:, 0:H], T.xin[:, 0:4 * H]), [("xin", 0, 4 * H)], [("qx", 0, H), ("sx", 0, H)])
    op("v", lambda: V.quantize_mx(T.qx[:, H:C], T.sx[:, H:C], T.xin[:, 4 * H:4 * C]), [("xin", 4 * H, 4 * C)], [("qx", H, C), ("sx", H, C)])
    scan("pkw", "pks", 0)
    pre = prep_p(0, P0)
    next(pre)
    op("v", lambda: V.quantize_mx(T.qe[:, :], T.se[:, :], T.ee[:, :]), [("ee", 0, 2048)] + [("ee%d" % b, 0, 128) for b in range(4)], [("qe", 0, 512), ("se", 0, 512)])

    def mm(bank, n, st, sts, a, mv, mvs, lo):
        op("t", lambda: g.tensor.matmul_mx(T["ps%d" % bank][:, 0:n], T[st][:, a:a + 128], T[sts][:, a:a + 128], T[mv][:, lo:lo + n], T[mvs][:, lo:lo + n], True, True),
           [(st, a, a + 128), (sts, a, a + 128), (mv, lo, lo + n), (mvs, lo, lo + n)], [("ps%d" % bank, 0, 512)])

    FB = [4, 5, 0, 1]

    def evac(q, bank, n, out, o, key, scale):
        src = T["ps%d" % bank][:, 0:n]
        dst = T[out][:, o:o + n]

        def make():
            if q == "s":
                return S.activation(dst, src, COPY) if scale is None else S.activation(dst, src, COPY, scale=scale)
            return V.tensor_copy(dst, src) if scale is None else V.tensor_scalar(dst, src, scale, None, MUL)
        op(q, make, [("ps%d" % bank, 0, 512)], [key])

    def gather_g(q, b, lu):
        src = T.fp[:, C * b:C * b + C].indirect(T[lu][:, 28:56])
        dst = T.gp[:, C * b:C * b + C]

        def make():
            if q == "s":
                return S.activation(dst, src, COPY, scale=0.5)
            return V.tensor_scalar(dst, src, 0.5, None, MUL)
        op(q, make, [("fp", C * b, C * b + C), (lu, 28, 56)], [("gp", C * b, C * b + C)])
        dma("y", T.g2[:, C * b:C * b + H], T.gp[:, C * b:C * b + H], "l_g%d" % b, [("gp", C * b, C * b + C)], [("g2", C * b, C * b + H)])

    def addend(b):
        d, s = T.g2[:, C * b + H:C * b + C], T.gp[:, C * b + H:C * b + C]
        R, W = [("gp", C * b, C * b + C)], [("g2", C * b + H, C * b + C)]
        if b < 2:
            op("g", lambda: g.affine_select(d, s, [[0, H]], GT, 0.0, 1, 0), R, W)
        else:
            cp(d, s, R, W)

    for t in range(3):
        last = t == 2
        lp, lu = "lu%d" % ((t - 1) % 4), "lu%d" % t
        ip_, in_ = "inv%d" % ((t - 1) % 3), "inv%d" % t
        dst = T.cores[rank ^ STEP[t]]
        rid, pid, _ = topo.addr(dst)
        eng = topo.engines(core, dst)
        d1 = T["d1%d" % t]
        for h in range(2):
            mm(2 + h, H, "qus", "sus", 0, "qx", "sx", H * h)
        for h in range(2):
            op("s", lambda: S.activation(T.sa[:, H * h:H * h + H], T["ps%d" % (2 + h)][:, 0:H], SIGN), [("ps%d" % (2 + h), 0, 512)], [("sa", H * h, H * h + H)])
        look("s", "h2", "sa", "pku")
        if t == 0:
            cp(T.lu3[:, 56:84], T.rfi[:, :], [("rfi", 0, 28)], [("lu3", 56, 84)])
            look("s", "fw", "iot", "lu3", 56, 84)
            look("s", "fkw", "fw", "ku", 0, 28)
        else:
            scan("fkw", "pks", C)
        rest = prep_f(t, F1 if t else F0)
        if t > 0:
            next(rest)
            next(rest)
        look("v", "h1", "sa", lp, 28, 56)
        if t == 0:
            next(pre)
            base("v", 0, 2, F0)
        scan("h1", "hs", 0, True)
        if t == 0:
            base("v", 0, 3, F0)
            base("v", 0, 1, P0)
            exchange(0)
            displace(0)
        scan("h2", "hs", C, True)
        for b in range(4):
            mm(FB[b], C, "qe", "se", 128 * b, "qx", "sx", 0)
        mm(6, C, "qus", "sus", 128, "qx", "sx", 0)
        for b in range(3):
            evac("s", FB[b], C, "fp", C * b, ("fp", C * b, C * b + C), None)
        op("s", lambda: S.activation(T.bs[:, :], T.ps6[:, 0:C], SIGN), [("ps6", 0, 512)], [tab("bs")])
        ts(T.fl[:, :], T.hs[:, 15:2 * C:16], TH, None, GE, None, [("hs", 0, 2 * C), RTH], [("fl", 0, 56)])
        if t > 0:
            next(rest)
        for i in range(4):
            tt(T.d0[:, 56 * i + 1:56 * i + 56:2], T.fl[:, 0:28], T.fl[:, 28:56], EQ, [("fl", 0, 56)], [("d0o%d" % i, 0, 28)])

        def select(i):
            op("v", lambda: V.tensor_tensor_scan(T.do[:, 112 * i:112 * i + 112], T.d0[:, 112 * i:112 * i + 112], d1[:, 112 * i:112 * i + 112], 0.0, MUL, ADD),
               [("d0", 0, 224), ("d0o%d" % (2 * i), 0, 28), ("d0o%d" % (2 * i + 1), 0, 28), ("d1d%d" % t, 56 * i, 56 * i + 56), ("d1b%d" % t, 56 * i, 56 * i + 56)],
               [("do", 112 * i, 112 * i + 112)])
        select(0)
        if t > 0:
            next(rest)
        cp(T[lu][:, 0:56], T.do[:, 1:112:2], [("do", 0, 112)], [(lu, 0, 56)])
        if not last:
            base("g", t + 1, 1, P1)
        if t == 0:
            scan("fkw", "pks", C)
        for _i in rest:
            pass
        select(1)
        evac("v", FB[3], C, "fp", C * 3, ("fp", C * 3, C * 4), None)
        cp(T.cu[:, :], T.do[:, 113:168:2], [("do", 112, 224)], [("cu", 0, 28)])
        look("s", "tw", "iot", lu, 0, 28)
        look("s", "tcw", "tw", "cu")
        look("s", "hb", "bs", lu, 28, 56)
        gather_g("v", 0, lu)
        copy("g", T.s31[:, 2:84:3], T.do[:, 169:224:2], [("do", 112, 224)], [("s31c", 0, 28)])
        if t == 0:
            ts(T.s30[:, 1:84:3], T.i28[:, 0:28], 0.0, SK, MUL, ADD, [RSK, Rio], [("s30", 0, 84)])
        ts(T.s31[:, 1:84:3], T.do[:, 169:224:2], -1.0, None, MUL, None, [("do", 112, 224)], [("s31b", 0, 28)])
        gather_g("v", 1, lu)
        addend(0)
        addend(1)
        gather_g("s", 2, lu)
        gather_g("s", 3, lu)
        scan("tcw", "tcs")
        scan("hb", "hbs", 0, True)
        cp(T.s31[:, 0:84:3], T.tcs[:, 15:C:16], [tab("tcs")], [("s31a", 0, 28)])
        ts(T.s30[:, 2:84:3], T.hbs[:, 15:C:16], TH, None, GE, None, [tab("hbs"), RTH], [("s30f", 0, 28)])
        op("v", lambda: V.tensor_tensor_scan(T.s3o[:, :], T.s30[:, :], T.s31[:, :], 0.0, MUL, ADD),
           [("s30", 0, 84), ("s30f", 0, 28), ("s31a", 0, 28), ("s31b", 0, 28), ("s31c", 0, 28)], [("s3o", 0, 84)])
        cp(T[lu][:, 56:84], T.s3o[:, 2:84:3], [("s3o", 0, 84)], [(lu, 56, 84)])
        need("g", [(lu, 56, 84)], [])
        fe = eng[0:8]
        g.remote_dma(T["fs%d" % t][:, :], T[lu][:, 56:84], T.sem["fr%d" % t], T.sem.loc, pid, rid, sum(1 << e for e in fe))
        total["loc"] = total.get("loc", 0) + len(fe)
        landed("fr%d" % t, len(fe), [("fs%d" % t, 0, 28)])
        qz, sz, qy, sy = "qzu%d" % t, "szu%d" % t, "qy%d" % t, "sy%d" % t
        addend(2)
        if not last:
            base("g", t + 1, 2, F1)
            base("g", t + 1, 3, F1)
        for h in (1, 0):
            for b in range(4):
                src = T.gp[:, C * b:C * b + C].indirect(T[lu][:, 56 + 14 * h:70 + 14 * h])
                tt(T.zt[:, 4 * H * h + b:4 * H * h + 4 * H:4], src, T.g2[:, C * b + H * h:C * b + H * h + H], ADD,
                   [("gp", C * b, C * b + C), (lu, 56, 84), ("g2", C * b + H * h, C * b + H * h + H)], [("zt%d" % b, H * h, H * h + H)])
                if h and b == 1:
                    addend(3)
            R = [("zt%d" % b, H * h, H * h + H) for b in range(4)]
            if not last:
                if h:
                    exchange(t + 1)
                else:
                    displace(t + 1)
            if h:
                op("v", lambda: V.quantize_mx(T[qz][:, :], T[sz][:, :], T.zt[:, 4 * H:4 * C]), R, [(qz, 0, H), (sz, 0, H)])
                need("g", [(qz, 0, H), (sz, 0, H)], [])
                to = [DstId(rid=rid, pnc=pid)]
                n = H // 4
                tr = []
                for i in range(4):
                    tr.append((T[qz][:, n * i:n * i + n].bitcast(dt.uint8), T[qy][:, H + n * i:H + n * i + n].bitcast(dt.uint8)))
                tr.append((T[sz][:, :], T[sy][:, H:C]))
                g.remote_dma_fused([RemoteDMATransfer(dst_ids=to, dma_engine_mask=sum(1 << e for e in eng[2 * i:2 * i + 2]), remote_sem=T.sem["zr%d" % t], src=a, dst=b)
                                    for i, (a, b) in enumerate(tr)], local_sem=T.sem.loc)
                total["loc"] += 10
                landed("zr%d" % t, 10, [(qy, H, C), (sy, H, C)])
            else:
                op("v", lambda: V.quantize_mx(T[qy][:, 0:H], T[sy][:, 0:H], T.zt[:, 0:4 * H]), R, [(qy, 0, H), (sy, 0, H)])
        if t == 0:
            op("v", lambda: V.tensor_copy(T.inw[:, 0:C].indirect(T[lu][:, 28:56]), T.iot[:, 0:C]), [(lu, 28, 56), tab("iot")], [tab("inw")])
        else:
            look("s", "inw", "tw", ip_)
        look("s", "pw", "iot", lu, 28, 56)
        if not last:
            look("s", "pkw", "pw", "ku", 28 * t + 28, 28 * t + 56)
        scan("inw", "ins")
        ts(T[in_][:, :], T.ins[:, 15:C:16], SK, None, MUL, None, [tab("ins"), RSK], [(in_, 0, 28)])
        look("s", "fsw", "iot", "fs%d" % t, 0, 28)
        look("s", "c2w", "fsw", lu, 56, 84)
        for b in range(4):
            mm(2 + b % 2, H, "qw", "sw", 128 * b, qy, sy, 0)
            if b == (0 if t == 1 else 2):
                look("s", "ew", "c2w", in_)
            evac("v" if (last and b > 1) or (t == 1 and b < 2) else "s", 2 + b % 2, H, "bp", C * b, ("bp", C * b, C * b + H), 0.03125)
        if not last:
            scan("pkw", "pks", 0)
            for _i in prep_p(t + 1, P1):
                pass
        else:
            dma("y", T.pf[:, 0:C], T.pw[0:128:16, :], "outy", [tab("pw")], [])
            op("v", lambda: V.quantize_mx(T.qv[:, :], T.sv[:, :], T.vt[:, :]), [("vt", 0, 512)], [("qv", 0, 128), ("sv", 0, 128)])
        scan("ew", "es")
        ts(T.eu[:, :], T.es[:, 15:C:16], SK, None, MUL, None, [tab("es"), RSK], [("eu", 0, 28)])
        for b in range(4):
            mm(4 + b, H, "qw", "sw", 128 * b, qy, sy, H)
            evac("s", 4 + b, H, "bp", C * b + H, ("bp", C * b + H, C * b + C), 0.03125)
        VP = 2 if last else 3
        for lo, hi in ([(0, CUT), (CUT, C)] if last else [(0, C)]):
            a, e = lo // 16, hi // 16
            for b in range(VP, 4):
                op("s", lambda: S.activation(T.tmp[:, C * (b - 2) + lo:C * (b - 2) + hi], T.bp[:, C * b:C * b + C].indirect(T.eu[:, a:e]), COPY),
                   [("bp", C * b, C * b + C), ("eu", 0, 28)], [("tmp", C * (b - 2) + lo, C * (b - 2) + hi)])
            if lo == 0:
                look("s", "fw", "iot", lu, 56, 84)
            if last and lo == 0:
                dma("y", T.pf[:, C:2 * C], T.fw[0:128:16, :], "outy", [tab("fw")], [])
            if not last:
                look("s", "fkw", "fw", "ku", 28 * t + 28, 28 * t + 56)
            for b in range(4):
                dst_ = T.xt[:, 4 * lo + b:4 * hi:4]
                if b < VP:
                    tt(dst_, T.bp[:, C * b:C * b + C].indirect(T.eu[:, a:e]), T.fp[:, C * b + lo:C * b + hi], ADD,
                       [("bp", C * b, C * b + C), ("eu", 0, 28), ("fp", C * b, C * b + C)], [("xt%d" % b, lo, hi)])
                else:
                    tt(dst_, T.tmp[:, C * (b - 2) + lo:C * (b - 2) + hi], T["ps%d" % FB[b]][:, lo:hi], ADD,
                       [("tmp", C * (b - 2) + lo, C * (b - 2) + hi), ("ps%d" % FB[b], 0, 512)], [("xt%d" % b, lo, hi)])
            for i, j in ([(lo, hi)] if last else [(0, H), (H, C)]):
                op("v", lambda: V.quantize_mx(T.qx[:, i:j], T.sx[:, i:j], T.xt[:, 4 * i:4 * j]),
                   [("xt%d" % b, lo, hi) for b in range(4)], [("qx", i, j), ("sx", i, j)])
            if last:
                mm(7 if lo else 6, hi - lo, "qv", "sv", 0, "qx", "sx", lo)
                dma("y", T.oc[:, 4 * lo:4 * hi], T.qx[:, lo:hi].bitcast(dt.uint8), "outy", [("qx", lo, hi)], [])
                if hi == C:
                    for i in range(4):
                        dma("y", T.osc[4 * i:4 * i + 4, :], T.sx[32 * i:32 * i + 4, :], "outy", [("sx", 0, C)], [])
        if last:
            for i, j, n in ((0, CUT, 6), (CUT, C, 7)):
                evac("s", n, j - i, "ysb", i, ("ysb", i, j), None)
                dma("s", T.y[:, i:j], T.ysb[:, i:j], "outs", [("ysb", i, j)], [])
    for sem in sorted(total):
        if waited.get(sem, 0) < total[sem]:
            g.wait_ge(T.sem[sem], total[sem])
